import numpy as np, ml_dtypes
CORES = [40,64,80,88,96,104,120,144]
N = 8
import mx_ref
BF = ml_dtypes.bfloat16
def pick(q, e):
    c = np.concatenate([q[0].reshape(128, -1, 4), np.zeros((128, 1, 4), np.uint8)], axis=1); s = np.concatenate([q[1], np.ones((16, 1), np.uint8)], axis=1)
    return (np.ascontiguousarray(c[:, e].reshape(128, -1)), np.ascontiguousarray(s[:, e]))
def join(*qs):
    return (np.concatenate([q[0] for q in qs], axis=1), np.concatenate([q[1] for q in qs], axis=1))
def put(q, e, v):
    c, s = q[0].reshape(128, -1, 4).copy(), q[1].copy(); c[:, e] = v[0].reshape(128, -1, 4); s[:, e] = v[1]
    return (c.reshape(128, -1), s)
def pk(c, s):
    return (np.ascontiguousarray(c), mx_ref.live(s))
def emit(q):
    return q[0], q[1]
def cut(t, i, w=512):
    return t[:, w * i:w * i + w]
def tile(rs):
    return np.stack(rs, axis=2).reshape(128, -1).astype(BF)
def f(rng, *shape):
    return mx_ref.flush((rng.standard_normal(shape, dtype=np.float32) * np.exp2(rng.integers(-2, 3, shape[:-1] + (1,)))).astype(BF))
def wide(rng, *shape, cols=0):
    v = rng.standard_normal(shape, dtype=np.float32) * np.exp2(rng.integers(-12, 13, shape)).astype(np.float32)
    if cols: v *= np.repeat(np.exp2(rng.integers(-cols, cols + 1, shape[:-2] + (1, shape[-1] // 4))) * (rng.random(shape[:-2] + (1, shape[-1] // 4)) > 0.0625), 4, axis=-1).astype(np.float32)
    return mx_ref.flush(v.astype(BF))
T, L, CAPP = 96, 3, 32
def game(x, u, w):
    S = [mx_ref.quantize(np.ascontiguousarray(x[r])) for r in range(N)]
    qu = [mx_ref.quantize(np.ascontiguousarray(u[r])) for r in range(N)]
    at, ks, made = np.arange(N * T).reshape(N, T), np.zeros((N, 1, L), np.float32), []
    for b in range(L):
        want = [np.flatnonzero(mx_ref.matmul(qu[r], S[r])[b] + np.float32(0) < 0) for r in range(N)]
        new, now = [], at.copy()
        for r in range(N):
            p = r ^ (1 << b)
            k = min(len(want[r]), len(want[p]), CAPP)
            to, of = want[r][:k], want[p][:k]
            c = pick(S[p], np.concatenate([of, np.full(CAPP - k, -1)]))
            t = tile([np.float32(0.0625) * mx_ref.matmul(mx_ref.quantize(np.ascontiguousarray(cut(w[r], 4 * b + i))), c) for i in range(4)])
            made.append(t)
            new.append(put(S[r], to, pick(mx_ref.quantize(t), np.arange(k))))
            now[r, to] = at[p, of]
            ks[r, 0, b] = k
        S, at = new, now
    return S, at, ks, made
def fit(t, low, high):
    a = np.abs(t.astype(np.float32))
    return bool((np.isfinite(a) & ((a == 0) | (a >= low) & (a <= high))).all())
def blocks(t):
    return np.abs(t.astype(np.float32)).reshape(16, 8, -1, 4).max(axis=(1, 3))
def plain(rng):
    u = np.array(f(rng, N, 128, 512))
    u[:, :, 4 * L:] = 0
    a = np.exp2(rng.integers(-2, 3, (N, 128, 1, 1)))
    x, lean = rng.standard_normal((N, 128, T, 4)), 2.5 * rng.random((N, L)) - 1
    for b in range(L):
        h = a * u[:, :, None, 4 * b:4 * b + 4].astype(np.float64)
        x += lean[:, b, None, None, None] * h * np.sum(h * h, axis=(1, 2, 3), keepdims=True) ** -0.5
    x = mx_ref.flush((a * x).reshape(N, 128, 4 * T).astype(np.float32).astype(BF))
    return {"x": x, "u": u, "w": f(rng, N, 128, 2048 * L), "v": f(rng, N, 128, 512)}
def aim(x, u, wish):
    x = x.reshape(N, 128, T, 4).astype(np.float32)
    for r in range(N):
        s = mx_ref.matmul(mx_ref.quantize(np.ascontiguousarray(u[r])), mx_ref.quantize(np.ascontiguousarray(x[r].reshape(128, 4 * T).astype(BF))))[0]
        x[r][:, s == 0] = u[r][:, None, :4].astype(np.float32)
        x[r][:, (s < 0) != wish[r]] *= -1
    return (x + np.float32(0)).reshape(N, 128, 4 * T).astype(BF)
def some(rng, n):
    return np.stack([rng.permutation(T) < n[r] for r in range(N)])
def setup_inputs(rng):
    return plain(rng)
def setup_inputs_many(rng):
    d = plain(rng)
    n = rng.integers(CAPP + 1, T + 1, N)
    j = 2 * int(rng.integers(0, N // 2))
    n[j:j + 2] = CAPP
    d["x"] = aim(d["x"], d["u"], some(rng, n))
    return d
def setup_inputs_none(rng):
    d = plain(rng)
    wish = some(rng, rng.integers(T // 4, T + 1, N))
    i, j = 2 * rng.permutation(N // 2)[:2] + rng.integers(0, 2, 2)
    wish[i] = False
    wish[i ^ 1] = True
    wish[j] = np.arange(T) == T - 1
    d["u"][int(rng.integers(0, N)), :, 4:8] = 0
    d["x"] = aim(d["x"], d["u"], wish)
    return d
def setup_inputs_zero(rng):
    d = plain(rng)
    d["u"][:, 64:, :4] = 0
    x = np.array(d["x"]).reshape(N, 128, T, 4)
    for r in range(N):
        e = rng.permutation(T)
        x[r][:, e[:T // 8]] = 0
        x[r][:64, e[T // 8:3 * T // 8]] = 0
    d["x"] = x.reshape(N, 128, 4 * T)
    return d
def setup_inputs_turn(rng):
    d = plain(rng)
    d["x"] = aim(d["x"], d["u"], some(rng, np.full(N, T // 2)))
    m, e = np.zeros((128, L, 4, 128, 4), np.float32), np.arange(128)
    for b in range(L):
        for i in range(4): m[e, b, i, e, i] = -16
    d["w"] = mx_ref.flush((m.reshape(128, 2048 * L) + d["w"].astype(np.float32) * np.float32(2.0 ** -6)).astype(BF))
    return d
def setup_inputs_spread(rng):
    d = plain(rng)
    u = np.array(wide(rng, N, 128, 512))
    u[:, :, 4 * L:] = 0
    return {**d, "x": wide(rng, N, 128, 4 * T, cols=6), "u": u, "v": wide(rng, N, 128, 512)}
def check_inputs(d):
    b = []
    for k in ("x", "u", "w", "v"):
        if not fit(d[k], 2.0 ** -30, 2.0 ** 30): b.append("a value of " + k)
    if (d["u"][:, :, 4 * L:].astype(np.float32) != 0).any(): b.append("u has numbers behind its first L columns")
    if not b:
        try:
            made = game(d["x"], d["u"], d["w"])[3]
            good, even = all(fit(t, 2.0 ** -60, 2.0 ** 60) for t in made), all(fit(blocks(t), 2.0 ** -30, 2.0 ** 30) for t in made)
        except Exception: good = even = False
        if not good: b.append("a number that an expert gives")
        if not even: b.append("the largest number of a block that an expert gives")
    return b
def reference(x, u, w, v):
    S, at, ks, made = game(x, u, w)
    oc, osc = np.zeros((N, 128, 4 * T), np.uint8), np.zeros((N, 16, T), np.uint8)
    y = np.zeros((N, 128, T), np.float32)
    for r in range(N):
        oc[r], osc[r] = emit(S[r])
        y[r] = mx_ref.matmul(mx_ref.quantize(np.ascontiguousarray(v[r])), S[r])
    return {"oc": oc, "osc": osc, "ids": at.reshape(N, 1, T).astype(np.float32), "ks": ks, "y": y}

@@ -1,0 +1,418 @@
+from concourse.bass import DstId, RemoteDMATransfer
+from concourse.mybir import dt, AluOpType, ActivationFunctionType
+
+PL, L, CAP = 96, 3, 32
+OP, AF = AluOpType, ActivationFunctionType
+F8, U8, F32, BF, U16, I32 = "float8_e4m3fn_x4", "uint8", "float32", "bfloat16", "uint16", "int32"
+BIG = 16384.0
+
+SCRATCH = {}
+
+
+def _buf(name, n, dtype, where="sbuf"):
+    SCRATCH[name] = (where, [128, n], dtype)
+
+
+def _pair(name, n):
+    _buf("q" + name, n, F8)
+    _buf("s" + name, n, U8)
+
+
+for _n, _w in (("xt", 512), ("ut", 512), ("vt", 512), ("zt", 512), ("wt0", 2048), ("wt1", 2048), ("wt2", 2048), ("h0", 512), ("h1", 512), ("h2", 512),
+               ("zc", 96 * L)):
+    _buf(_n, _w, BF)
+for _n, _w in (("u", 128), ("g0", 128), ("g1", 128), ("g2", 128), ("w0", 512), ("w1", 512), ("w2", 512), ("v", 128),
+               ("b0", 128), ("b1", 224), ("b2", 224), ("f", 96), ("d0", 224), ("d1", 224), ("d2", 224), ("e0", 128), ("e1", 128), ("e2", 128)):
+    _pair(_n, _w)
+for _n in ("psa", "pse", "pr0", "pr1", "pr2", "pr3"):
+    _buf(_n, 512, F32, "psum")
+for _n, _w in (("t16", 96), ("p18", 18), ("cc", 4), ("mk", 96), ("rs", 96), ("zz", 96), ("dd0", 12 * L), ("dd1", 12 * L), ("so", 12 * L),
+               ("wn", 96 * L), ("nw", 96 * L), ("jk", 96 * L), ("jk2", 96 * L), ("acc", 2 * L), ("cw", 96 * L), ("dg", 96 * L),
+               ("ds", 96 * L), ("t6", 6 * L), ("ov", 6 * L), ("dx", 6 * L), ("fe0", 128), ("fe1", 128), ("fe2", 128), ("fw0", 128), ("fw1", 128), ("fw2", 128),
+               ("idp", 128), ("iw0", 128), ("iw1", 128), ("iw2", 128), ("idl", 96), ("si1", 32), ("si2", 32), ("sit1", 32), ("sit2", 32),
+               ("rb1", 32), ("rb2", 32), ("km", 3), ("ksb", 3), ("yb", 96)):
+    _buf(_n, _w, F32)
+_buf("iq", 2, I32)
+_buf("iqa", 2, I32)
+_buf("cf", 8 * L, U16)
+_buf("mo", 8 * L, U16)
+_buf("lo", 2 * L, U16)
+_buf("ll", 2 * L, U16)
+_buf("ko", L, BF)
+_buf("mine", L, U16)
+_buf("his", L, U16)
+for _b in range(L):
+    _buf("xa%d" % _b, 48, F8)
+    _buf("xb%d" % _b, 48, F8)
+    _buf("xs%d" % _b, 96, U8)
+_buf("xks", L, BF)
+_buf("xis", L, U16)
+_buf("xls", 2 * L, U16)
+
+FLOWS = {}
+for _b in range(L):
+    FLOWS["a%d" % _b] = (0, _b, "xa%d" % _b, 0, "qd%d" % _b, 0, 48)
+    FLOWS["b%d" % _b] = (2, _b, "xb%d" % _b, 0, "qd%d" % _b, 48, 48)
+    FLOWS["s%d" % _b] = (1, _b, "xs%d" % _b, 0, "sd%d" % _b, 0, 96)
+    FLOWS["k%d" % _b] = (0, _b, "xks", _b, "ko", _b, 1)
+    FLOWS["l%d" % _b] = (0, _b, "xls", 2 * _b, "ll", 2 * _b, 2)
+    if _b:
+        FLOWS["i%d" % _b] = (1, _b, "xis", _b, "his", _b, 1)
+ORDER = (("a0", "k0", "l0", "a1", "k1", "l1", "a2", "k2", "l2"), ("s0", "s1", "i1", "s2", "i2"), ("b0", "b1", "b2"))
+
+VCH, SCH = ["va", "vc", "ve", "vf", "vp", "vi", "vq", "vk", "vm", "vt"], ["s1", "s2", "s3", "s4"]
+SEMAPHORES = (["a_" + f for f in FLOWS] + VCH + SCH + ["st", "r0", "r1", "r2", "r3", "sq", "sg", "sh", "lsa", "ls0", "ls1", "ls2", "lx", "lu", "lv",
+              "oy", "oc1", "oc2", "oi", "ok"] + ["lw%d%d" % (_b, _i) for _b in range(L) for _i in range(4)])
+
+
+def _raw(view, name):
+    return view.bitcast(dt.uint8) if SCRATCH[name][2] == F8 else view
+
+
+def _mask(es):
+    return sum(1 << e for e in es)
+
+
+def _relays(core, T, topo):
+    r = T.rank_of(core)
+    ps = [T.cores[r ^ (1 << b)] for b in range(L)]
+    rel = [c for c in topo.cores_of(core) if c != core and all(topo.may_write(c, p) for p in ps)]
+    rel.sort(key=lambda c: (topo.die(c) != topo.die(core), c))
+    return rel[:3], ps
+
+
+def _hop1(f, src, dst, topo):
+    es = topo.engines(src, dst)
+    h = len(es) // 2
+    return es[:h] if f[0] == "a" else es[h:] if f[0] == "b" else es
+
+
+def _relay_program(g, core, me, partners, T, topo, rankcore):
+    sent = 0
+    for f in ORDER[me]:
+        _, lev, xb, xa, db, a, w = FLOWS[f]
+        g.wait_ge(T.sem["a_" + f], len(_hop1(f, rankcore, core, topo)))
+        dst = partners[lev]
+        rid, pid = topo.addr(dst, core)
+        es = topo.engines(core, dst)
+        g.remote_dma(_raw(T[db][:, a:a + w], db), _raw(T[xb][:, xa:xa + w], xb), T.sem["a_" + f], T.sem.lsa, pid, rid, _mask(es))
+        sent += len(es)
+    g.wait_ge(T.sem.lsa, sent)
+
+
+def rank_program(g, core, T, topo):
+    rank = T.rank_of(core)
+    if rank is None:
+        for rc in T.cores:
+            if rc in topo.cores_of(core):
+                rel, partners = _relays(rc, T, topo)
+                if core in rel:
+                    _relay_program(g, core, rel.index(core), partners, T, topo, rc)
+        return
+    rel, partners = _relays(core, T, topo)
+    cnt = {}
+    seen = {}
+    vec = g.vector
+
+    def need(q, eng, toks):
+        best = {}
+        for s, n in toks:
+            if seen.get((q, s), 0) < n:
+                best[s] = max(n, best.get(s, 0))
+        for s in best:
+            eng.wait_ge(T.sem[s], best[s])
+            seen[(q, s)] = best[s]
+
+    def bump(s, ins, n=1):
+        ins.then_inc(T.sem[s], n)
+        cnt[s] = cnt.get(s, 0) + n
+        return (s, cnt[s])
+
+    def now(*names):
+        return [(s, cnt[s]) for s in (names or VCH + SCH) if cnt.get(s)]
+
+    def V(ch, call, *args, deps=(), free=False, **kw):
+        s = "v" + ch
+        need("v", vec, list(deps) + ([] if free else now(s)))
+        return bump(s, call(*args, **kw))
+
+    def S(ch, *args, deps=(), **kw):
+        need("s", g.scalar, list(deps) + now(ch))
+        return bump(ch, g.scalar.activation(*args, **kw))
+
+    def MM(s, out, l, r, deps):
+        need("t", g.tensor, deps)
+        (ln, la), (rn, ra) = l, r
+        return bump(s, g.tensor.matmul_mx(out[:, 0:128], T["q" + ln][:, la:la + 128], T["s" + ln][:, la:la + 128],
+                                          T["q" + rn][:, ra:ra + 128], T["s" + rn][:, ra:ra + 128], True, True))
+
+    def DMA(eng, q, s, out, in_, deps=()):
+        need(q, eng, deps)
+        return bump(s, eng.dma_start(out, in_), 16)
+
+    def pick_s(out, a, win, off, w, deps=()):
+        return S("s1", T["s" + out][:, a:a + w], T["s" + win][:, 0:128].indirect(off), AF.Copy, deps=deps)
+
+    def pick_v(ch, out, a, win, off, w, deps=()):
+        return V(ch, vec.tensor_copy, T["q" + out][:, a:a + w].bitcast(dt.uint32), T["q" + win][:, 0:128].bitcast(dt.uint32).indirect(off), deps=deps)
+
+    def hop1(f, name, a, b):
+        k, _, xb, xa, _, _, w = FLOWS[f]
+        rid, pid = topo.addr(rel[k], core)
+        return rid, pid, _hop1(f, core, rel[k], topo), _raw(T[xb][:, xa:xa + w], xb), _raw(T[name][:, a:b], name)
+
+    def left(b):
+        return ("ls%d" % b, cnt["ls%d" % b])
+
+    def send(f, name, a, b, deps):
+        need("g", g, deps)
+        rid, pid, es, out, in_ = hop1(f, name, a, b)
+        ls = "ls%d" % FLOWS[f][1]
+        g.remote_dma(out, in_, T.sem["a_" + f], T.sem[ls], pid, rid, _mask(es))
+        cnt[ls] = cnt.get(ls, 0) + len(es)
+
+    def send2(parts, deps):
+        need("g", g, deps)
+        tr = []
+        for f, name, a, b in parts:
+            rid, pid, es, out, in_ = hop1(f, name, a, b)
+            ls = "ls%d" % FLOWS[f][1]
+            tr.append(RemoteDMATransfer(dst_ids=[DstId(rid=rid, pnc=pid)], dma_engine_mask=_mask(es), remote_sem=T.sem["a_" + f], srcs=[in_], dsts=[out]))
+            cnt[ls] = cnt.get(ls, 0) + len(es)
+        g.remote_dma_fused(tr, local_sem=T.sem[ls])
+
+    def arr(f):
+        src = _relays(partners[FLOWS[f][1]], T, topo)[0][FLOWS[f][0]]
+        return ("a_" + f, len(topo.engines(src, core)))
+
+    def columns(b, tq, ts):
+        send2([("a%d" % b, "qb%d" % b, 0, 48), ("b%d" % b, "qb%d" % b, 48, 96)], [tq])
+        send("s%d" % b, "sb%d" % b, 0, 96, [ts])
+
+    def c(name, b, w=PL):
+        return T[name][:, w * b:w * b + w]
+
+    def mo(b):
+        return T.mo[:, 8 * b:8 * b + 6]
+
+    def ll(b):
+        return T.ll[:, 2 * b:2 * b + 2]
+
+    t_u = DMA(g.sync, "y", "lu", T.ut[:, 0:16], T.u[:, 0:16])
+    t_x = DMA(g.scalar, "s", "lx", T.xt[:, 0:4 * PL], T.x[:, 0:4 * PL])
+
+    def load_w(b, deps=()):
+        return [DMA(g.sync, "y", "lw%d%d" % (b, i), T["wt%d" % b][:, 512 * i:512 * i + 512], T.w[:, 2048 * b + 512 * i:2048 * b + 512 * i + 512], deps)
+                for i in range(4)]
+    t_lw = [load_w(0), None, None]
+
+    def iota(s, view, pattern, base, cm):
+        return bump(s, g.iota(view, pattern, base, cm, allow_small_or_imprecise_dtypes=True))
+    t_iq = bump("sq", g.iota(T.iq[:, 0:2], [[0, 2]], 0, 1))
+    iota("sg", T.t16[:, 0:96], [[0, 6], [1, 16]], 0, 0)
+    t_io = iota("sg", T.p18[:, 0:18], [[0, 3], [16, 6]], 0, 0)
+
+    V("k", vec.memset, T.ut[:, 16:512], 0.0, free=True)
+    V("k", vec.memset, T.cf[:, 0:8], 0, free=True)
+    V("k", vec.memset, T.xt[:, 384:512], 0.0, free=True)
+    V("k", vec.memset, T.zz[:, :], 0.0, free=True)
+    t_k = now("vk")
+    ic, jb0, jb1 = T.cc[:, 0:1], T.cc[:, 1:2], T.cc[:, 2:3]
+    V("c", vec.tensor_scalar, T.iqa[:, :], T.iq[:, :], 15, None, OP.bitwise_and, deps=[t_iq])
+    V("k", vec.memset, T.zt[:, :], 0.0, free=True)
+    t_ic = V("c", vec.tensor_copy, ic, T.iqa[:, 0:1])
+    V("k", vec.memset, T.cf[:, 8:16], 1, free=True)
+    V("k", vec.memset, T.cf[:, 16:24], 2, free=True)
+    V("t", vec.tensor_scalar, jb0, ic, 256.0, 128.0, OP.mult, OP.add, deps=[t_ic])
+    t_jc = V("t", vec.tensor_scalar, jb1, ic, 256.0, 4224.0, OP.mult, OP.add, free=True)
+    V("k", vec.memset, T.dd0[:, :], 0.0, free=True)
+    V("k", vec.memset, T.h0[:, 384:512], 0.0, free=True)
+    t_qu = V("a", vec.quantize_mx, T.qu[:, :], T.su[:, :], T.ut[:, :], deps=[t_u] + t_k)
+    t_qb = V("q", vec.quantize_mx, T.qb0[:, :], T.sb0[:, :], T.xt[:, :], deps=[t_x])
+
+    def gauge(b, ch):
+        off = T.cf[:, 8 * b:8 * b + 8]
+        s = pick_s("g%d" % b, 0, "u", off, 128, [t_qu] + now("vk"))
+        return [pick_v(ch, "g%d" % b, 0, "u", off, 128, [t_qu] + now("vk")), s]
+    t_g = [gauge(0, "a"), None, None]
+    columns(0, t_qb, t_qb)
+    t_mm = MM("st", T.psa, ("g0", 0), ("b0", 0), t_g[0] + [t_qb])
+
+    def zeros(*names):
+        for n in names:
+            V("q", vec.quantize_mx, T["q" + n][:, 96:224], T["s" + n][:, 96:224], T.zt[:, :], deps=now("vk"), free=True)
+
+    def make_list(b, t_wn, gap1, gap2):
+        t_zc = V("a", vec.tensor_tensor_scan, c("zc", b), c("wn", b), T.zz[:, :], 0.0, OP.add, OP.add)
+        a0 = S("s2", c("jk", b), c("zc", b), AF.Sign, bias=jb0, scale=-1.0, accum_out=T.acc[:, 2 * b:2 * b + 1], deps=[t_zc, t_jc])
+        a1 = S("s3", c("jk2", b), c("zc", b), AF.Sign, bias=jb1, scale=-1.0, accum_out=T.acc[:, 2 * b + 1:2 * b + 2])
+        t_nw = S("s4", c("nw", b), c("wn", b), AF.Identity, bias=BIG, scale=-BIG / 256, deps=[t_wn])
+        send("k%d" % b, "zc", 96 * b + 95, 96 * b + 96, [t_zc])
+        gap1()
+        t_lo = V("a", vec.tensor_scalar, T.lo[:, 2 * b:2 * b + 2], T.acc[:, 2 * b:2 * b + 2], 96.0, 0.5, OP.add, OP.mult, deps=[a0, a1])
+        send("l%d" % b, "lo", 2 * b, 2 * b + 2, [t_lo])
+        gap2(t_lo)
+        return t_zc, t_nw
+
+    def prep(b, t_zc, t_nw):
+        ds, d1 = T.ds[:, 96 * b + 15:96 * b + 96:16], T.dd1[:, 12 * b:12 * b + 12:2]
+        t = []
+
+        def small():
+            d = now("vp")
+            t.append(S("s4", c("t6", b, 6), ds, AF.Identity, bias=PL - 1.0, scale=1.0 / 256, deps=d))
+            t.append(S("s2", c("ov", b, 6), ds, AF.Relu, scale=64.0, bias=T.cc[:, 3:4], deps=d + now("vt")))
+
+        def last():
+            V("p", vec.tensor_tensor, d1, c("t6", b, 6), T.dd1[:, 12 * b + 1:12 * b + 12:2], OP.subtract, deps=t[:1])
+            V("p", vec.tensor_tensor, c("dx", b, 6), c("ov", b, 6), ds, OP.add, deps=t[1:], free=True)
+        return [lambda: V("p", vec.tensor_tensor, c("cw", b), c("zc", b), c("nw", b), OP.add, deps=[t_zc, t_nw]),
+                lambda: V("p", vec.tensor_tensor, c("dg", b), c("cw", b), T.mk[:, :], OP.mult, deps=now("vt")),
+                lambda: V("p", vec.tensor_tensor_scan, c("ds", b), T.rs[:, :], c("dg", b), 0.0, OP.mult, OP.add),
+                small, last]
+
+    def merge_list(b):
+        return [lambda: V("m", vec.tensor_scalar, T.dd0[:, 12 * b + 1:12 * b + 12:2], c("dx", b, 6), T.ko[:, b:b + 1], None, OP.is_le,
+                          deps=[arr("k%d" % b)] + now("vp", "vk")),
+                lambda: V("m", vec.tensor_tensor_scan, c("so", b, 12), c("dd0", b, 12), c("dd1", b, 12), 0.0, OP.mult, OP.add),
+                lambda: V("m", vec.tensor_copy, T.mo[:, 8 * b:8 * b + 6], T.so[:, 12 * b + 1:12 * b + 12:2])]
+
+    def quant_w(b, i):
+        return V("q", vec.quantize_mx, T["qw%d" % b][:, 128 * i:128 * i + 128], T["sw%d" % b][:, 128 * i:128 * i + 128],
+                 T["wt%d" % b][:, 512 * i:512 * i + 512], deps=[t_lw[b][i]], free=True)
+
+    def expert(b, tw, deps, m):
+        h, n = T["h%d" % b], PL
+        tr = [MM("r%d" % i, T["pr%d" % i], ("w%d" % b, 128 * i), ("d%d" % b, 0), deps + [tw[i]]) for i in range(4)]
+        t0 = S("s1", h[:, 0:4 * n:4], T.pr0[:, 0:n], AF.Copy, scale=0.0625, deps=[tr[0]])
+        t2 = S("s2", h[:, 2:4 * n:4], T.pr2[:, 0:n], AF.Copy, scale=0.0625, deps=[tr[2]])
+        t1 = V("e", vec.tensor_scalar, h[:, 1:4 * n:4], T.pr1[:, 0:n], 0.0625, None, OP.mult, deps=[tr[1]], free=True)
+        t3 = V("e", vec.tensor_scalar, h[:, 3:4 * n:4], T.pr3[:, 0:n], 0.0625, None, OP.mult, deps=[tr[3]], free=True)
+        t_r = [t0, t1, t2, t3]
+        t_e = V("e", vec.quantize_mx, T["qe%d" % b][:, :], T["se%d" % b][:, :], T["h%d" % b][:, :], deps=t_r + [t_io2] + now("vk"))
+        m[0]()
+        m[1]()
+        return t_r, t_e
+
+    def flags(buf, n, ps, deps):
+        return V("f", vec.tensor_scalar, T[buf][:, 0:n], ps[:, 0:n], 0.0, 256.0, OP.is_lt, OP.mult, deps=deps, free=True)
+
+    def row_numbers(b, deps):
+        return S("s3", T["iw%d" % (b + 1)][:, 0:96], T["iw%d" % b][:, :].indirect(mo(b)), AF.Copy, deps=deps)
+
+    def give_numbers(b, t_lo):
+        t = S("s3", T["si%d" % b][:, :], T["iw%d" % b][:, :].indirect(T.lo[:, 2 * b:2 * b + 2]), AF.Copy, deps=[t_lo])
+
+        def out():
+            send("i%d" % b, "mine", b, b + 1, [V("i", vec.tensor_copy, T.mine[:, b:b + 1], T["sit%d" % b][:, 0:1])])
+        return [lambda: V("i", vec.transpose, T["sit%d" % b][:, :], T["si%d" % b][:, :], deps=[t]), out]
+
+    def take_numbers(b):
+        return [lambda: V("i", vec.tensor_copy, T["rb%d" % b][:, 0:1], T.his[:, b:b + 1], deps=[arr("i%d" % b), t_io2]),
+                lambda: V("i", vec.transpose, T["iw%d" % b][:, 96:128], T["rb%d" % b][:, :])]
+
+    zeros("d0")
+    t_wn = V("a", vec.tensor_scalar, c("wn", 0), T.psa[:, 0:96], 0.0, 256.0, OP.is_lt, OP.mult, deps=[t_mm])
+
+    def consts():
+        V("t", vec.tensor_scalar, T.mk[:, :], T.t16[:, :], ic, None, OP.is_equal, deps=[t_io], free=True)
+        V("t", vec.tensor_scalar, T.rs[:, :], T.t16[:, :], 0.0, None, OP.is_gt, free=True)
+        V("t", vec.tensor_scalar, T.dd1[:, 1:12 * L:2], T.p18[:, :], ic, None, OP.add, free=True)
+        V("t", vec.memset, T.cc[:, 3:4], -64.0 * 256 * CAP, free=True)
+    t_zn = make_list(0, t_wn, consts, lambda t: None)
+    for b in (1, 2):
+        iota("sh", T["h%d" % b][:, 384:512], [[0, 128]], 0, 0)
+        iota("sh", T["rb%d" % b][:, :], [[0, 32]], 0, 0)
+        iota("sh", T["iw%d" % b][:, 96:128], [[0, 32]], 0, 0)
+    iota("sh", T.iw0[:, 0:96], [[1, 96]], rank * PL, 0)
+    t_io2 = iota("sh", T.idp[:, 0:128], [[1, 128]], T.rank_of(partners[0]) * PL, 0)
+    t_lw[1] = load_w(1, [left(0)])
+    t_v = DMA(g.sync, "y", "lv", T.vt[:, :], T.v[:, :])
+
+    p = prep(0, *t_zn)
+    p[0]()
+    t_g[1] = gauge(1, "q")
+    t_mm = MM("st", T.psa, ("g1", 0), ("b0", 0), t_g[1] + [t_qb, t_wn])
+    p[1]()
+    p[2]()
+    p[3]()
+    t_w = [quant_w(0, 0)]
+    t_fo = flags("fw0", 96, T.psa, [t_mm])
+    t_w.append(quant_w(0, 1))
+    p[4]()
+    t_w += [quant_w(0, 2), quant_w(0, 3)]
+    t_g[2] = gauge(2, "q")
+    zeros("d1", "b1")
+    m = merge_list(0)
+    t_r, t_e = expert(0, t_w, [arr("a0"), arr("b0"), arr("s0")], m)
+
+    t_qv = []
+    for b in range(L):
+        nxt = ("g%d" % (b + 1), 0) if b < 2 else ("v", 0)
+        t_se = MM("st", T.pse, nxt, ("e%d" % b, 0), [t_e, t_fo] + (t_g[b + 1] if b < 2 else t_qv))
+        off = ll(b)
+        t_cs = pick_s("b%d" % b, 96, "e%d" % b, off, 32, [t_e, t_fo, arr("l%d" % b)] + now("vq"))
+        t_cv = pick_v("c", "b%d" % b, 96, "e%d" % b, off, 32, [t_e, t_fo, arr("l%d" % b)] + now("vq"))
+        t_mo = m[2]()
+        if b == 0:
+            t_new = S("s3", T.iw0[:, 96:128], T.idp[:, :].indirect(off), AF.Copy, deps=[t_io2])
+        if b < 2:
+            t_fe = flags("fe%d" % b, 128, T.pse, [t_se])
+        else:
+            t_fe = S("s2", T.fe2[:, :], T.pse[:, 0:128], AF.Copy, deps=[t_se])
+        nb = "b%d" % (b + 1) if b < 2 else "f"
+        t_ss = pick_s(nb, 0, "b%d" % b, mo(b), 96, [t_cs, t_mo])
+        t_sv = pick_v("c", nb, 0, "b%d" % b, mo(b), 96, [t_cv, t_mo])
+        t_fn = V("f", vec.tensor_copy, T["fw%d" % b][:, 96:128], T["fe%d" % b][:, :].indirect(off), deps=[t_fe])
+        if b == 2:
+            break
+        columns(b + 1, t_sv, t_ss)
+        t_wn = V("a", vec.tensor_copy, c("wn", b + 1), T["fw%d" % b][:, :].indirect(mo(b)), deps=[t_fn, t_fo, t_mo])
+        give = []
+        if b == 0:
+            def gap1():
+                row_numbers(0, [t_new, t_mo])
+                zeros("d2", "b2")
+        else:
+            take = take_numbers(1)
+
+            def gap1():
+                take[0]()
+                t_qv.append(V("q", vec.quantize_mx, T.qv[:, :], T.sv[:, :], T.vt[:, :], deps=[t_v], free=True))
+                take[1]()
+                row_numbers(1, now("vi") + [t_mo])
+        t_zn = make_list(b + 1, t_wn, gap1, lambda t: give.extend(give_numbers(b + 1, t)))
+        t_mm = MM("st", T.psa, ("g2", 0) if b == 0 else ("v", 0), ("b%d" % (b + 1), 0), (t_g[2] if b == 0 else t_qv) + [t_sv, t_ss, t_fo] + now("vq"))
+        p = prep(b + 1, *t_zn)
+        p[0]()
+        t_w = [quant_w(b + 1, 0)]
+        p[1]()
+        give[0]()
+        t_w.append(quant_w(b + 1, 1))
+        p[2]()
+        give[1]()
+        if b == 0:
+            t_lw[2] = load_w(2, [left(1)])
+        p[3]()
+        t_w += [quant_w(b + 1, 2), quant_w(b + 1, 3)]
+        if b == 0:
+            t_fo = flags("fw1", 96, T.psa, [t_mm])
+        else:
+            t_fo = V("f", vec.tensor_copy, T.fw2[:, 0:96], T.psa[:, 0:96], deps=[t_mm], free=True)
+        p[4]()
+        m = merge_list(b + 1)
+        t_r, t_e = expert(b + 1, t_w, t_r + [arr("%s%d" % (f, b + 1)) for f in "abs"], m)
+
+    t_y = V("a", vec.tensor_copy, T.yb[:, :], T.fw2[:, :].indirect(mo(2)), deps=[t_fn, t_fo, t_mo])
+    for k in range(4):
+        DMA(g.sync, "y", "oc2", T.osc[4 * k:4 * k + 4, 0:PL], T.sf[32 * k:32 * k + 4, 0:96], [t_ss])
+    DMA(g.scalar, "s", "oc1", T.oc[:, 0:4 * PL], T.qf[:, 0:96].bitcast(dt.uint8), [t_sv])
+    DMA(g.sync, "y", "oy", T.y[:, :], T.yb[:, :], [t_y])
+    for f in take_numbers(2):
+        f()
+    t_id = S("s3", T.idl[:, :], T.iw2[:, :].indirect(mo(2)), AF.Copy, deps=now("vi"))
+    DMA(g.scalar, "s", "oi", T.ids[0:1, :], T.idl[0:1, :], [t_id])
+    V("f", vec.tensor_tensor, T.km[:, :], T.zc[:, 95:96 * L:96], T.ko[:, :], OP.min, deps=now("va"))
+    t_ks = V("f", vec.tensor_scalar, T.ksb[:, :], T.km[:, :], 256.0 * CAP, 1.0 / 256, OP.min, OP.mult)
+    DMA(g.sync, "y", "ok", T.ks[0:1, :], T.ksb[0:1, :], [t_ks])
+    need("g", g, [(s, n) for s, n in cnt.items() if n] + [arr(f) for f in FLOWS])

@@ -2,9 +2,9 @@ from concourse.bass import DstId, RemoteDMATransfer
 from concourse.mybir import dt, AluOpType, ActivationFunctionType
 
 PL, L, CAP = 96, 3, 32
+W = PL + CAP
 OP, AF = AluOpType, ActivationFunctionType
 F8, U8, F32, BF, U16, I32 = "float8_e4m3fn_x4", "uint8", "float32", "bfloat16", "uint16", "int32"
-BIG = 16384.0
 
 SCRATCH = {}
 
@@ -18,19 +18,19 @@ def _pair(name, n):
     _buf("s" + name, n, U8)
 
 
-for _n, _w in (("xt", 512), ("ut", 512), ("vt", 512), ("zt", 512), ("wt0", 2048), ("wt1", 2048), ("wt2", 2048), ("h0", 512), ("h1", 512), ("h2", 512),
-               ("zc", 96 * L)):
+for _n, _w in (("xt", 512), ("vt", 512), ("zt", 512), ("wt0", 2048), ("wt1", 2048), ("wt2", 2048), ("h0", 512), ("h1", 512), ("h2", 512),
+               ("zc", W * L), ("wn", W), ("ex", W)):
     _buf(_n, _w, BF)
-for _n, _w in (("u", 128), ("g0", 128), ("g1", 128), ("g2", 128), ("w0", 512), ("w1", 512), ("w2", 512), ("v", 128),
-               ("b0", 128), ("b1", 224), ("b2", 224), ("f", 96), ("d0", 224), ("d1", 224), ("d2", 224), ("e0", 128), ("e1", 128), ("e2", 128)):
+for _n, _w in (("g0", 128), ("g1", 128), ("g2", 128), ("w0", 512), ("w1", 512), ("w2", 512), ("v", 128),
+               ("b0", 128), ("b1", 128), ("b2", 128), ("c0", 128), ("c1", 224), ("c2", 224), ("c3", 224),
+               ("d0", 224), ("d1", 224), ("d2", 224), ("e0", 160), ("e1", 160), ("e2", 160)):
     _pair(_n, _w)
-for _n in ("psa", "pse", "pr0", "pr1", "pr2", "pr3"):
+for _n in ("psa", "pr0", "pr1", "pr2", "pr3"):
     _buf(_n, 512, F32, "psum")
-for _n, _w in (("t16", 96), ("p18", 18), ("cc", 4), ("mk", 96), ("rs", 96), ("zz", 96), ("dd0", 12 * L), ("dd1", 12 * L), ("so", 12 * L),
-               ("wn", 96 * L), ("nw", 96 * L), ("jk", 96 * L), ("jk2", 96 * L), ("acc", 2 * L), ("cw", 96 * L), ("dg", 96 * L),
-               ("ds", 96 * L), ("t6", 6 * L), ("ov", 6 * L), ("dx", 6 * L), ("fe0", 128), ("fe1", 128), ("fe2", 128), ("fw0", 128), ("fw1", 128), ("fw2", 128),
-               ("idp", 128), ("iw0", 128), ("iw1", 128), ("iw2", 128), ("idl", 96), ("si1", 32), ("si2", 32), ("sit1", 32), ("sit2", 32),
-               ("rb1", 32), ("rb2", 32), ("km", 3), ("ksb", 3), ("yb", 96)):
+for _n, _w in (("t16", 96), ("row", W), ("cc", 4), ("mk", 96), ("rs", 96), ("one", W), ("jk", W * L), ("jk2", W * L), ("jk3", CAP * L), ("acc", 2 * L),
+               ("mr0", W), ("mr1", W), ("mr2", W), ("ds", 96 * L),
+               ("ia0", W), ("ia", W), ("iw0", W), ("iw1", W), ("iw2", W), ("ih", W), ("im", 96), ("idl", 96),
+               ("sit1", 32), ("sit2", 32), ("rb", 32), ("his", L), ("km", L), ("ksb", L), ("yb", 96)):
     _buf(_n, _w, F32)
 _buf("iq", 2, I32)
 _buf("iqa", 2, I32)
@@ -38,31 +38,26 @@ _buf("cf", 8 * L, U16)
 _buf("mo", 8 * L, U16)
 _buf("lo", 2 * L, U16)
 _buf("ll", 2 * L, U16)
-_buf("ko", L, BF)
-_buf("mine", L, U16)
-_buf("his", L, U16)
 for _b in range(L):
     _buf("xa%d" % _b, 48, F8)
     _buf("xb%d" % _b, 48, F8)
-    _buf("xs%d" % _b, 96, U8)
-_buf("xks", L, BF)
-_buf("xis", L, U16)
+    _buf("xs%d" % _b, PL, U8)
+_buf("xis", L, F32)
 _buf("xls", 2 * L, U16)
 
 FLOWS = {}
 for _b in range(L):
     FLOWS["a%d" % _b] = (0, _b, "xa%d" % _b, 0, "qd%d" % _b, 0, 48)
     FLOWS["b%d" % _b] = (2, _b, "xb%d" % _b, 0, "qd%d" % _b, 48, 48)
-    FLOWS["s%d" % _b] = (1, _b, "xs%d" % _b, 0, "sd%d" % _b, 0, 96)
-    FLOWS["k%d" % _b] = (0, _b, "xks", _b, "ko", _b, 1)
+    FLOWS["s%d" % _b] = (1, _b, "xs%d" % _b, 0, "sd%d" % _b, 0, PL)
     FLOWS["l%d" % _b] = (0, _b, "xls", 2 * _b, "ll", 2 * _b, 2)
     if _b:
         FLOWS["i%d" % _b] = (1, _b, "xis", _b, "his", _b, 1)
-ORDER = (("a0", "k0", "l0", "a1", "k1", "l1", "a2", "k2", "l2"), ("s0", "s1", "i1", "s2", "i2"), ("b0", "b1", "b2"))
+ORDER = (("a0", "l0", "a1", "l1", "a2", "l2"), ("s0", "s1", "i1", "s2", "i2"), ("b0", "b1", "b2"))
 
-VCH, SCH = ["va", "vc", "ve", "vf", "vp", "vi", "vq", "vk", "vm", "vt"], ["s1", "s2", "s3", "s4"]
-SEMAPHORES = (["a_" + f for f in FLOWS] + VCH + SCH + ["st", "r0", "r1", "r2", "r3", "sq", "sg", "sh", "lsa", "ls0", "ls1", "ls2", "lx", "lu", "lv",
-              "oy", "oc1", "oc2", "oi", "ok"] + ["lw%d%d" % (_b, _i) for _b in range(L) for _i in range(4)])
+VCH, SCH = ["va", "vc", "ve", "vf", "vp", "vi", "vq", "vk", "vo", "vt", "vz"], ["s1", "s2", "s3", "s4"]
+SEMAPHORES = (["a_" + f for f in FLOWS] + VCH + SCH + ["st", "r0", "r1", "r2", "r3", "sq", "sg", "sh", "lsa", "ls0", "ls1", "ls2", "li1", "li2", "lx", "lv",
+              "oy", "oc1", "oc2", "oi", "ok", "lw0a", "lw0b", "lw1", "lw2a", "lw2b"])
 
 
 def _raw(view, name):
@@ -71,6 +66,10 @@ def _raw(view, name):
 
 def _mask(es):
     return sum(1 << e for e in es)
+
+
+def _landed(f):
+    return "a_a" + f[1] if f[0] in "abs" else "a_" + f
 
 
 def _relays(core, T, topo):
@@ -95,7 +94,7 @@ def _relay_program(g, core, me, partners, T, topo, rankcore):
         dst = partners[lev]
         rid, pid = topo.addr(dst, core)
         es = topo.engines(core, dst)
-        g.remote_dma(_raw(T[db][:, a:a + w], db), _raw(T[xb][:, xa:xa + w], xb), T.sem["a_" + f], T.sem.lsa, pid, rid, _mask(es))
+        g.remote_dma(_raw(T[db][:, a:a + w], db), _raw(T[xb][:, xa:xa + w], xb), T.sem[_landed(f)], T.sem.lsa, pid, rid, _mask(es))
         sent += len(es)
     g.wait_ge(T.sem.lsa, sent)
 
@@ -129,15 +128,15 @@ def rank_program(g, core, T, topo):
         return (s, cnt[s])
 
     def now(*names):
-        return [(s, cnt[s]) for s in (names or VCH + SCH) if cnt.get(s)]
+        return [(s, cnt[s]) for s in names if cnt.get(s)]
 
     def V(ch, call, *args, deps=(), free=False, **kw):
         s = "v" + ch
-        need("v", vec, list(deps) + ([] if free else now(s)))
+        need("v", vec, ([] if free else now(s)) + list(deps))
         return bump(s, call(*args, **kw))
 
-    def S(ch, *args, deps=(), **kw):
-        need("s", g.scalar, list(deps) + now(ch))
+    def S(ch, *args, deps=(), free=False, **kw):
+        need("s", g.scalar, ([] if free else now(ch)) + list(deps))
         return bump(ch, g.scalar.activation(*args, **kw))
 
     def MM(s, out, l, r, deps):
@@ -150,269 +149,269 @@ def rank_program(g, core, T, topo):
         need(q, eng, deps)
         return bump(s, eng.dma_start(out, in_), 16)
 
-    def pick_s(out, a, win, off, w, deps=()):
-        return S("s1", T["s" + out][:, a:a + w], T["s" + win][:, 0:128].indirect(off), AF.Copy, deps=deps)
+    def pick_s(ch, out, a, win, wa, off, w, deps=()):
+        return S(ch, T["s" + out][:, a:a + w], T["s" + win][:, wa:wa + 128].indirect(off), AF.Copy, deps=deps)
 
-    def pick_v(ch, out, a, win, off, w, deps=()):
-        return V(ch, vec.tensor_copy, T["q" + out][:, a:a + w].bitcast(dt.uint32), T["q" + win][:, 0:128].bitcast(dt.uint32).indirect(off), deps=deps)
+    def pick_v(ch, out, a, win, wa, off, w, deps=(), free=False):
+        return V(ch, vec.tensor_copy, T["q" + out][:, a:a + w].bitcast(dt.uint32), T["q" + win][:, wa:wa + 128].bitcast(dt.uint32).indirect(off),
+                 deps=deps, free=free)
 
-    def hop1(f, name, a, b):
-        k, _, xb, xa, _, _, w = FLOWS[f]
+    def hop1(f, name, a):
+        k, lev, xb, xa, _, _, w = FLOWS[f]
         rid, pid = topo.addr(rel[k], core)
-        return rid, pid, _hop1(f, core, rel[k], topo), _raw(T[xb][:, xa:xa + w], xb), _raw(T[name][:, a:b], name)
+        es = _hop1(f, core, rel[k], topo)
+        gone = ("li%d" if f[0] == "i" else "ls%d") % lev
+        cnt[gone] = cnt.get(gone, 0) + len(es)
+        return rid, pid, _mask(es), _raw(T[xb][:, xa:xa + w], xb), _raw(T[name][:, a:a + w], name), gone
 
-    def left(b):
-        return ("ls%d" % b, cnt["ls%d" % b])
-
-    def send(f, name, a, b, deps):
+    def send(f, name, a, deps):
         need("g", g, deps)
-        rid, pid, es, out, in_ = hop1(f, name, a, b)
-        ls = "ls%d" % FLOWS[f][1]
-        g.remote_dma(out, in_, T.sem["a_" + f], T.sem[ls], pid, rid, _mask(es))
-        cnt[ls] = cnt.get(ls, 0) + len(es)
+        rid, pid, m, out, in_, gone = hop1(f, name, a)
+        g.remote_dma(out, in_, T.sem["a_" + f], T.sem[gone], pid, rid, m)
 
     def send2(parts, deps):
         need("g", g, deps)
         tr = []
-        for f, name, a, b in parts:
-            rid, pid, es, out, in_ = hop1(f, name, a, b)
-            ls = "ls%d" % FLOWS[f][1]
-            tr.append(RemoteDMATransfer(dst_ids=[DstId(rid=rid, pnc=pid)], dma_engine_mask=_mask(es), remote_sem=T.sem["a_" + f], srcs=[in_], dsts=[out]))
-            cnt[ls] = cnt.get(ls, 0) + len(es)
-        g.remote_dma_fused(tr, local_sem=T.sem[ls])
+        for f, name, a in parts:
+            rid, pid, m, out, in_, gone = hop1(f, name, a)
+            tr.append(RemoteDMATransfer(dst_ids=[DstId(rid=rid, pnc=pid)], dma_engine_mask=m, remote_sem=T.sem["a_" + f], srcs=[in_], dsts=[out]))
+        g.remote_dma_fused(tr, local_sem=T.sem[gone])
 
-    def arr(f):
-        src = _relays(partners[FLOWS[f][1]], T, topo)[0][FLOWS[f][0]]
-        return ("a_" + f, len(topo.engines(src, core)))
+    def arr(*fs):
+        src = _relays(partners[FLOWS[fs[0]][1]], T, topo)[0]
+        return (_landed(fs[0]), sum(len(topo.engines(src[FLOWS[f][0]], core)) for f in fs))
+
+    def cols(b):
+        return arr("a%d" % b, "b%d" % b, "s%d" % b)
 
     def columns(b, tq, ts):
-        send2([("a%d" % b, "qb%d" % b, 0, 48), ("b%d" % b, "qb%d" % b, 48, 96)], [tq])
-        send("s%d" % b, "sb%d" % b, 0, 96, [ts])
+        send2([("a%d" % b, "qc%d" % b, 0), ("b%d" % b, "qc%d" % b, 48)], [tq])
+        send("s%d" % b, "sc%d" % b, 0, [ts])
 
-    def c(name, b, w=PL):
+    def c(name, b, w=W):
         return T[name][:, w * b:w * b + w]
 
     def mo(b):
         return T.mo[:, 8 * b:8 * b + 6]
 
+    def lo(b):
+        return T.lo[:, 2 * b:2 * b + 2]
+
     def ll(b):
         return T.ll[:, 2 * b:2 * b + 2]
 
-    t_u = DMA(g.sync, "y", "lu", T.ut[:, 0:16], T.u[:, 0:16])
-    t_x = DMA(g.scalar, "s", "lx", T.xt[:, 0:4 * PL], T.x[:, 0:4 * PL])
+    DMA(g.sync, "y", "lx", T.xt[:, 0:4 * PL], T.x[:, 0:4 * PL])
+    t_x = DMA(g.scalar, "s", "lx", T.xt[:, 4 * PL:4 * PL + 16], T.u[:, 0:16])
 
-    def load_w(b, deps=()):
-        return [DMA(g.sync, "y", "lw%d%d" % (b, i), T["wt%d" % b][:, 512 * i:512 * i + 512], T.w[:, 2048 * b + 512 * i:2048 * b + 512 * i + 512], deps)
-                for i in range(4)]
-    t_lw = [load_w(0), None, None]
+    def load_w(s, b, i, n, deps=()):
+        return [DMA(g.sync, "y", s, T["wt%d" % b][:, 512 * i:512 * (i + n)], T.w[:, 2048 * b + 512 * i:2048 * b + 512 * (i + n)], deps)] * n
+    t_lw = [load_w("lw0a", 0, 0, 2) + load_w("lw0b", 0, 2, 2), None, None]
 
     def iota(s, view, pattern, base, cm):
         return bump(s, g.iota(view, pattern, base, cm, allow_small_or_imprecise_dtypes=True))
-    t_iq = bump("sq", g.iota(T.iq[:, 0:2], [[0, 2]], 0, 1))
-    iota("sg", T.t16[:, 0:96], [[0, 6], [1, 16]], 0, 0)
-    t_io = iota("sg", T.p18[:, 0:18], [[0, 3], [16, 6]], 0, 0)
 
-    V("k", vec.memset, T.ut[:, 16:512], 0.0, free=True)
-    V("k", vec.memset, T.cf[:, 0:8], 0, free=True)
-    V("k", vec.memset, T.xt[:, 384:512], 0.0, free=True)
-    V("k", vec.memset, T.zz[:, :], 0.0, free=True)
-    t_k = now("vk")
-    ic, jb0, jb1 = T.cc[:, 0:1], T.cc[:, 1:2], T.cc[:, 2:3]
+    def nought(view, n):
+        return iota("sh", view, [[0, n]], 0, 0)
+    t_iq = bump("sq", g.iota(T.iq[:, 0:2], [[0, 2]], 0, 1))
+    t_row = iota("sg", T.row[:, :], [[1, W]], 0, 0)
+    t_io = iota("sg", T.t16[:, 0:96], [[0, 6], [1, 16]], 0, 0)
+
+    def fill(view, val):
+        return V("k", vec.memset, view, val, free=True)
+    fill(T.xt[:, 4 * PL + 16:512], 0.0)
+    fill(T.cf[:, 0:8], PL)
+    fill(T.wn[:, PL:W], 0.0)
+    ic, jb0, jb1, back = T.cc[:, 0:1], T.cc[:, 1:2], T.cc[:, 2:3], T.cc[:, 3:4]
     V("c", vec.tensor_scalar, T.iqa[:, :], T.iq[:, :], 15, None, OP.bitwise_and, deps=[t_iq])
-    V("k", vec.memset, T.zt[:, :], 0.0, free=True)
+    fill(T.ex[:, 0:PL], 0.0)
+    fill(T.h0[:, 0:128], 0.0)
     t_ic = V("c", vec.tensor_copy, ic, T.iqa[:, 0:1])
-    V("k", vec.memset, T.cf[:, 8:16], 1, free=True)
-    V("k", vec.memset, T.cf[:, 16:24], 2, free=True)
-    V("t", vec.tensor_scalar, jb0, ic, 256.0, 128.0, OP.mult, OP.add, deps=[t_ic])
-    t_jc = V("t", vec.tensor_scalar, jb1, ic, 256.0, 4224.0, OP.mult, OP.add, free=True)
-    V("k", vec.memset, T.dd0[:, :], 0.0, free=True)
-    V("k", vec.memset, T.h0[:, 384:512], 0.0, free=True)
-    t_qu = V("a", vec.quantize_mx, T.qu[:, :], T.su[:, :], T.ut[:, :], deps=[t_u] + t_k)
-    t_qb = V("q", vec.quantize_mx, T.qb0[:, :], T.sb0[:, :], T.xt[:, :], deps=[t_x])
+    t_z = fill(T.zt[:, :], 0.0)
+    V("t", vec.tensor_scalar, jb0, ic, 0.5, None, OP.add, deps=[t_ic])
+    t_jc = V("t", vec.tensor_scalar, jb1, ic, 16.5, None, OP.add, free=True)
+    V("k", vec.tensor_copy, T.ex[:, PL:W], T.row[:, 1:CAP + 1], deps=[t_row], free=True)
+    t_k = now("vk")
+
+    t_qc = V("c", vec.quantize_mx, T.qc0[:, :], T.sc0[:, :], T.xt[:, :], deps=t_k + [t_x])
+    columns(0, t_qc, t_qc)
 
     def gauge(b, ch):
         off = T.cf[:, 8 * b:8 * b + 8]
-        s = pick_s("g%d" % b, 0, "u", off, 128, [t_qu] + now("vk"))
-        return [pick_v(ch, "g%d" % b, 0, "u", off, 128, [t_qu] + now("vk")), s]
+        s = pick_s("s4", "g%d" % b, 0, "c0", 0, off, 128, now("vk") + [t_qc])
+        return [pick_v(ch, "g%d" % b, 0, "c0", 0, off, 128, now("vk") + [t_qc]), s]
+    V("o", vec.quantize_mx, T.qb0[:, :], T.sb0[:, :], T.xt[:, :], free=True)
     t_g = [gauge(0, "a"), None, None]
-    columns(0, t_qb, t_qb)
-    t_mm = MM("st", T.psa, ("g0", 0), ("b0", 0), t_g[0] + [t_qb])
 
     def zeros(*names):
         for n in names:
-            V("q", vec.quantize_mx, T["q" + n][:, 96:224], T["s" + n][:, 96:224], T.zt[:, :], deps=now("vk"), free=True)
+            V("z", vec.quantize_mx, T["q" + n][:, 96:224], T["s" + n][:, 96:224], T.zt[:, :], deps=[t_z], free=True)
 
-    def make_list(b, t_wn, gap1, gap2):
-        t_zc = V("a", vec.tensor_tensor_scan, c("zc", b), c("wn", b), T.zz[:, :], 0.0, OP.add, OP.add)
-        a0 = S("s2", c("jk", b), c("zc", b), AF.Sign, bias=jb0, scale=-1.0, accum_out=T.acc[:, 2 * b:2 * b + 1], deps=[t_zc, t_jc])
-        a1 = S("s3", c("jk2", b), c("zc", b), AF.Sign, bias=jb1, scale=-1.0, accum_out=T.acc[:, 2 * b + 1:2 * b + 2])
-        t_nw = S("s4", c("nw", b), c("wn", b), AF.Identity, bias=BIG, scale=-BIG / 256, deps=[t_wn])
-        send("k%d" % b, "zc", 96 * b + 95, 96 * b + 96, [t_zc])
+    def make_list(b, deps, gap0, gap1, gap2):
+        t_mm = MM("st", T.psa, ("g%d" % b, 0), ("c%d" % b, 0), deps)
+        gap0()
+        V("a", vec.tensor_scalar, T.wn[:, 0:PL], T.psa[:, 0:PL], 0.0, None, OP.is_lt, deps=[t_mm])
         gap1()
-        t_lo = V("a", vec.tensor_scalar, T.lo[:, 2 * b:2 * b + 2], T.acc[:, 2 * b:2 * b + 2], 96.0, 0.5, OP.add, OP.mult, deps=[a0, a1])
-        send("l%d" % b, "lo", 2 * b, 2 * b + 2, [t_lo])
-        gap2(t_lo)
-        return t_zc, t_nw
+        t_zc = V("a", vec.tensor_tensor_scan, c("zc", b), T.wn[:, :], T.ex[:, :], 0.0, OP.add, OP.max)
+        a0 = S("s2", c("jk", b), c("zc", b), AF.Sign, bias=jb0, scale=-1.0, accum_out=T.acc[:, 2 * b:2 * b + 1], deps=[t_jc, t_zc], free=True)
+        a1 = S("s2", c("jk2", b), c("zc", b), AF.Sign, bias=jb1, scale=-1.0, accum_out=T.acc[:, 2 * b + 1:2 * b + 2], free=True)
+        gap2()
+        t_lo = V("a", vec.tensor_scalar, lo(b), T.acc[:, 2 * b:2 * b + 2], float(W), 0.5, OP.add, OP.mult, deps=[a0, a1])
+        send("l%d" % b, "lo", 2 * b, [t_lo])
+        return t_lo
 
-    def prep(b, t_zc, t_nw):
-        ds, d1 = T.ds[:, 96 * b + 15:96 * b + 96:16], T.dd1[:, 12 * b:12 * b + 12:2]
-        t = []
+    def merge_list(b, t_lo):
+        mr = T["mr%d" % b]
+        return [lambda: V("p", vec.tensor_copy, mr[:, :].indirect(lo(b)), T.row[:, PL:W], deps=now("vt", "sh") + [t_lo]),
+                lambda: V("p", vec.tensor_tensor_scan, c("ds", b, PL), T.rs[:, :], mr[:, 0:PL], 0.0, OP.add, OP.max),
+                lambda: V("p", vec.tensor_scalar, mo(b), T.ds[:, 96 * b + 15:96 * b + 96:16], back, None, OP.add)]
 
-        def small():
-            d = now("vp")
-            t.append(S("s4", c("t6", b, 6), ds, AF.Identity, bias=PL - 1.0, scale=1.0 / 256, deps=d))
-            t.append(S("s2", c("ov", b, 6), ds, AF.Relu, scale=64.0, bias=T.cc[:, 3:4], deps=d + now("vt")))
+    def own(b, t_lo):
+        pick_v("o", "e%d" % b, 128, "c%d" % b, 0, lo(b), CAP, [t_lo], free=True)
+        pick_s("s4", "e%d" % b, 128, "c%d" % b, 0, lo(b), CAP, [t_lo])
 
-        def last():
-            V("p", vec.tensor_tensor, d1, c("t6", b, 6), T.dd1[:, 12 * b + 1:12 * b + 12:2], OP.subtract, deps=t[:1])
-            V("p", vec.tensor_tensor, c("dx", b, 6), c("ov", b, 6), ds, OP.add, deps=t[1:], free=True)
-        return [lambda: V("p", vec.tensor_tensor, c("cw", b), c("zc", b), c("nw", b), OP.add, deps=[t_zc, t_nw]),
-                lambda: V("p", vec.tensor_tensor, c("dg", b), c("cw", b), T.mk[:, :], OP.mult, deps=now("vt")),
-                lambda: V("p", vec.tensor_tensor_scan, c("ds", b), T.rs[:, :], c("dg", b), 0.0, OP.mult, OP.add),
-                small, last]
+    def quant_w(b, *tiles):
+        for i in tiles:
+            V("q", vec.quantize_mx, T["qw%d" % b][:, 128 * i:128 * i + 128], T["sw%d" % b][:, 128 * i:128 * i + 128],
+              T["wt%d" % b][:, 512 * i:512 * i + 512], deps=[t_lw[b][i]], free=True)
 
-    def merge_list(b):
-        return [lambda: V("m", vec.tensor_scalar, T.dd0[:, 12 * b + 1:12 * b + 12:2], c("dx", b, 6), T.ko[:, b:b + 1], None, OP.is_le,
-                          deps=[arr("k%d" % b)] + now("vp", "vk")),
-                lambda: V("m", vec.tensor_tensor_scan, c("so", b, 12), c("dd0", b, 12), c("dd1", b, 12), 0.0, OP.mult, OP.add),
-                lambda: V("m", vec.tensor_copy, T.mo[:, 8 * b:8 * b + 6], T.so[:, 12 * b + 1:12 * b + 12:2])]
-
-    def quant_w(b, i):
-        return V("q", vec.quantize_mx, T["qw%d" % b][:, 128 * i:128 * i + 128], T["sw%d" % b][:, 128 * i:128 * i + 128],
-                 T["wt%d" % b][:, 512 * i:512 * i + 512], deps=[t_lw[b][i]], free=True)
-
-    def expert(b, tw, deps, m):
+    def expert(b, deps):
         h, n = T["h%d" % b], PL
-        tr = [MM("r%d" % i, T["pr%d" % i], ("w%d" % b, 128 * i), ("d%d" % b, 0), deps + [tw[i]]) for i in range(4)]
-        t0 = S("s1", h[:, 0:4 * n:4], T.pr0[:, 0:n], AF.Copy, scale=0.0625, deps=[tr[0]])
-        t2 = S("s2", h[:, 2:4 * n:4], T.pr2[:, 0:n], AF.Copy, scale=0.0625, deps=[tr[2]])
-        t1 = V("e", vec.tensor_scalar, h[:, 1:4 * n:4], T.pr1[:, 0:n], 0.0625, None, OP.mult, deps=[tr[1]], free=True)
-        t3 = V("e", vec.tensor_scalar, h[:, 3:4 * n:4], T.pr3[:, 0:n], 0.0625, None, OP.mult, deps=[tr[3]], free=True)
-        t_r = [t0, t1, t2, t3]
-        t_e = V("e", vec.quantize_mx, T["qe%d" % b][:, :], T["se%d" % b][:, :], T["h%d" % b][:, :], deps=t_r + [t_io2] + now("vk"))
-        m[0]()
-        m[1]()
-        return t_r, t_e
+        tr = [MM("r%d" % i, T["pr%d" % i], ("w%d" % b, 128 * i), ("d%d" % b, 0), deps + [cols(b)]) for i in range(4)]
+        S("s1", h[:, 128:512:4], T.pr0[:, 0:n], AF.Copy, scale=0.0625, deps=[tr[0]])
+        t2 = S("s1", h[:, 130:512:4], T.pr2[:, 0:n], AF.Copy, scale=0.0625, deps=[tr[2]], free=True)
+        need("s", g.scalar, now("vo", "vp", "s4"))
+        V("e", vec.tensor_scalar, h[:, 129:512:4], T.pr1[:, 0:n], 0.0625, None, OP.mult, deps=[tr[1]], free=True)
+        t3 = V("e", vec.tensor_scalar, h[:, 131:512:4], T.pr3[:, 0:n], 0.0625, None, OP.mult, deps=[tr[3]], free=True)
+        need("v", vec, now("vk", "vo", "vp", "vc") + t_h[b])
+        t_e = V("e", vec.quantize_mx, T["qe%d" % b][:, 0:128], T["se%d" % b][:, 0:128], h[:, :], deps=[t2, t3], free=True)
+        return [t2, t3], t_e
 
-    def flags(buf, n, ps, deps):
-        return V("f", vec.tensor_scalar, T[buf][:, 0:n], ps[:, 0:n], 0.0, 256.0, OP.is_lt, OP.mult, deps=deps, free=True)
+    def ia(b):
+        return T.ia if b else T.ia0
 
-    def row_numbers(b, deps):
-        return S("s3", T["iw%d" % (b + 1)][:, 0:96], T["iw%d" % b][:, :].indirect(mo(b)), AF.Copy, deps=deps)
+    def own_numbers(b, t_lo, deps):
+        return S("s3", ia(b)[:, PL:W], T["iw%d" % b][:, :].indirect(lo(b)), AF.Copy, deps=deps + [t_lo])
 
-    def give_numbers(b, t_lo):
-        t = S("s3", T["si%d" % b][:, :], T["iw%d" % b][:, :].indirect(T.lo[:, 2 * b:2 * b + 2]), AF.Copy, deps=[t_lo])
+    def give_numbers(b, t):
+        send("i%d" % b, "sit%d" % b, 0, [V("i", vec.transpose, T["sit%d" % b][:, :], T.ia[:, PL:W], deps=[t])])
 
-        def out():
-            send("i%d" % b, "mine", b, b + 1, [V("i", vec.tensor_copy, T.mine[:, b:b + 1], T["sit%d" % b][:, 0:1])])
-        return [lambda: V("i", vec.transpose, T["sit%d" % b][:, :], T["si%d" % b][:, :], deps=[t]), out]
+    def new_numbers(b, deps):
+        S("s3", T["iw%d" % b][:, PL:W], ia(b)[:, :].indirect(ll(b)), AF.Copy, deps=deps)
 
-    def take_numbers(b):
-        return [lambda: V("i", vec.tensor_copy, T["rb%d" % b][:, 0:1], T.his[:, b:b + 1], deps=[arr("i%d" % b), t_io2]),
-                lambda: V("i", vec.transpose, T["iw%d" % b][:, 96:128], T["rb%d" % b][:, :])]
+    def kept_numbers(b):
+        return S("s3", T.im[:, :] if b else T.iw1[:, 0:PL], T["iw%d" % b][:, :].indirect(mo(b)), AF.Copy)
 
-    zeros("d0")
-    t_wn = V("a", vec.tensor_scalar, c("wn", 0), T.psa[:, 0:96], 0.0, 256.0, OP.is_lt, OP.mult, deps=[t_mm])
+    def count(b):
+        return S("s4", c("jk3", b, CAP), T.one[:, :].indirect(ll(b)), AF.Copy, accum_out=T.km[:, b:b + 1], deps=now("vt"), free=True)
+
+    def take_numbers(b, t_kept):
+        out = T.iw2[:, 0:PL] if b == 1 else T.idl[:, :]
+        return [lambda: V("i", vec.tensor_copy, T.rb[:, 0:1], T.his[:, b:b + 1], deps=t_ih + [arr("i%d" % b)]),
+                lambda: V("i", vec.transpose, T.ih[:, PL:W], T.rb[:, :]),
+                lambda: V("i", vec.tensor_tensor, out, T.ih[:, :].indirect(mo(b)), T.im[:, :], OP.add, deps=[t_kept])]
 
     def consts():
-        V("t", vec.tensor_scalar, T.mk[:, :], T.t16[:, :], ic, None, OP.is_equal, deps=[t_io], free=True)
-        V("t", vec.tensor_scalar, T.rs[:, :], T.t16[:, :], 0.0, None, OP.is_gt, free=True)
-        V("t", vec.tensor_scalar, T.dd1[:, 1:12 * L:2], T.p18[:, :], ic, None, OP.add, free=True)
-        V("t", vec.memset, T.cc[:, 3:4], -64.0 * 256 * CAP, free=True)
-    t_zn = make_list(0, t_wn, consts, lambda t: None)
-    for b in (1, 2):
-        iota("sh", T["h%d" % b][:, 384:512], [[0, 128]], 0, 0)
-        iota("sh", T["rb%d" % b][:, :], [[0, 32]], 0, 0)
-        iota("sh", T["iw%d" % b][:, 96:128], [[0, 32]], 0, 0)
-    iota("sh", T.iw0[:, 0:96], [[1, 96]], rank * PL, 0)
-    t_io2 = iota("sh", T.idp[:, 0:128], [[1, 128]], T.rank_of(partners[0]) * PL, 0)
-    t_lw[1] = load_w(1, [left(0)])
-    t_v = DMA(g.sync, "y", "lv", T.vt[:, :], T.v[:, :])
+        t = V("t", vec.tensor_scalar, T.mk[:, :], T.t16[:, :], ic, -64.0 * W, OP.is_equal, OP.mult, deps=[t_io], free=True)
+        V("t", vec.tensor_copy, T.mr0[:, :], T.row[:, :], free=True)
+        V("t", vec.tensor_scalar, back, ic, -15.0, float(W), OP.add, OP.mult, free=True)
+        V("t", vec.tensor_scalar, T.rs[:, :], T.mk[:, :], float(W), None, OP.add, deps=[t], free=True)
+        V("t", vec.tensor_scalar, T.one[:, :], T.row[:, :], float(PL), None, OP.is_lt, free=True)
 
-    p = prep(0, *t_zn)
+    def offsets():
+        fill(T.cf[:, 8:16], PL + 1)
+        fill(T.cf[:, 16:24], PL + 2)
+    t_lo = make_list(0, [t_qc] + t_g[0], lambda: zeros("d0", "c1", "d1"), offsets, consts)
+    t_lw[1] = load_w("lw1", 1, 0, 4, now("ls0"))
+    t_lw[2] = load_w("lw2a", 2, 0, 2)
+
+    p = merge_list(0, t_lo)
+    quant_w(0, 0)
     p[0]()
-    t_g[1] = gauge(1, "q")
-    t_mm = MM("st", T.psa, ("g1", 0), ("b0", 0), t_g[1] + [t_qb, t_wn])
+    iota("sh", T.iw0[:, :], [[1, W]], rank * PL, 0)
+    t_i0 = iota("sh", T.ia0[:, 0:PL], [[1, PL]], T.rank_of(partners[0]) * PL, 0)
+    t_h = [[], [nought(T.h1[:, 0:128], 128)]]
+    nought(T.iw1[:, PL:W], CAP)
+    iota("sh", T.mr1[:, :], [[1, W]], 0, 0)
+    quant_w(0, 1)
     p[1]()
+    quant_w(0, 2, 3)
+    t_w = now("vq", "vz")
     p[2]()
-    p[3]()
-    t_w = [quant_w(0, 0)]
-    t_fo = flags("fw0", 96, T.psa, [t_mm])
-    t_w.append(quant_w(0, 1))
-    p[4]()
-    t_w += [quant_w(0, 2), quant_w(0, 3)]
-    t_g[2] = gauge(2, "q")
-    zeros("d1", "b1")
-    m = merge_list(0)
-    t_r, t_e = expert(0, t_w, [arr("a0"), arr("b0"), arr("s0")], m)
+    own(0, t_lo)
+    t_g[1] = gauge(1, "f")
+    own_numbers(0, t_lo, [t_i0])
+    t_r, t_e = expert(0, t_w)
+    t_ia, t_ih = [], []
 
-    t_qv = []
     for b in range(L):
-        nxt = ("g%d" % (b + 1), 0) if b < 2 else ("v", 0)
-        t_se = MM("st", T.pse, nxt, ("e%d" % b, 0), [t_e, t_fo] + (t_g[b + 1] if b < 2 else t_qv))
-        off = ll(b)
-        t_cs = pick_s("b%d" % b, 96, "e%d" % b, off, 32, [t_e, t_fo, arr("l%d" % b)] + now("vq"))
-        t_cv = pick_v("c", "b%d" % b, 96, "e%d" % b, off, 32, [t_e, t_fo, arr("l%d" % b)] + now("vq"))
-        t_mo = m[2]()
-        if b == 0:
-            t_new = S("s3", T.iw0[:, 96:128], T.idp[:, :].indirect(off), AF.Copy, deps=[t_io2])
-        if b < 2:
-            t_fe = flags("fe%d" % b, 128, T.pse, [t_se])
-        else:
-            t_fe = S("s2", T.fe2[:, :], T.pse[:, 0:128], AF.Copy, deps=[t_se])
-        nb = "b%d" % (b + 1) if b < 2 else "f"
-        t_ss = pick_s(nb, 0, "b%d" % b, mo(b), 96, [t_cs, t_mo])
-        t_sv = pick_v("c", nb, 0, "b%d" % b, mo(b), 96, [t_cv, t_mo])
-        t_fn = V("f", vec.tensor_copy, T["fw%d" % b][:, 96:128], T["fe%d" % b][:, :].indirect(off), deps=[t_fe])
+        d = [arr("l%d" % b), t_e]
+        pick_s("s1", "b%d" % b, PL, "e%d" % b, CAP, ll(b), CAP, d)
+        pick_v("c", "b%d" % b, PL, "e%d" % b, CAP, ll(b), CAP, d)
+        new_numbers(b, t_ia)
+        need("t", g.tensor, now("vz", "va", "vq") + (t_g[b + 1] if b < 2 else []))
+        t_ss = pick_s("s1", "c%d" % (b + 1), 0, "b%d" % b, 0, mo(b), PL)
+        t_sv = pick_v("c", "c%d" % (b + 1), 0, "b%d" % b, 0, mo(b), PL)
         if b == 2:
             break
         columns(b + 1, t_sv, t_ss)
-        t_wn = V("a", vec.tensor_copy, c("wn", b + 1), T["fw%d" % b][:, :].indirect(mo(b)), deps=[t_fn, t_fo, t_mo])
-        give = []
-        if b == 0:
-            def gap1():
-                row_numbers(0, [t_new, t_mo])
-                zeros("d2", "b2")
-        else:
-            take = take_numbers(1)
+        t_n = [kept_numbers(b)]
+        take = take_numbers(1, t_n[0])
 
-            def gap1():
+        def gap0():
+            pick_s("s4", "b%d" % (b + 1), 0, "b%d" % b, 0, mo(b), PL)
+            count(b)
+            quant_w(b + 1, 0, 1)
+            if b == 1:
                 take[0]()
-                t_qv.append(V("q", vec.quantize_mx, T.qv[:, :], T.sv[:, :], T.vt[:, :], deps=[t_v], free=True))
-                take[1]()
-                row_numbers(1, now("vi") + [t_mo])
-        t_zn = make_list(b + 1, t_wn, gap1, lambda t: give.extend(give_numbers(b + 1, t)))
-        t_mm = MM("st", T.psa, ("g2", 0) if b == 0 else ("v", 0), ("b%d" % (b + 1), 0), (t_g[2] if b == 0 else t_qv) + [t_sv, t_ss, t_fo] + now("vq"))
-        p = prep(b + 1, *t_zn)
-        p[0]()
-        t_w = [quant_w(b + 1, 0)]
-        p[1]()
-        give[0]()
-        t_w.append(quant_w(b + 1, 1))
-        p[2]()
-        give[1]()
-        if b == 0:
-            t_lw[2] = load_w(2, [left(1)])
-        p[3]()
-        t_w += [quant_w(b + 1, 2), quant_w(b + 1, 3)]
-        if b == 0:
-            t_fo = flags("fw1", 96, T.psa, [t_mm])
-        else:
-            t_fo = V("f", vec.tensor_copy, T.fw2[:, 0:96], T.psa[:, 0:96], deps=[t_mm], free=True)
-        p[4]()
-        m = merge_list(b + 1)
-        t_r, t_e = expert(b + 1, t_w, t_r + [arr("%s%d" % (f, b + 1)) for f in "abs"], m)
 
-    t_y = V("a", vec.tensor_copy, T.yb[:, :], T.fw2[:, :].indirect(mo(2)), deps=[t_fn, t_fo, t_mo])
+        def gap1():
+            if b == 1:
+                take[1]()
+
+        def gap2():
+            if b == 1:
+                t_n.append(take[2]())
+            quant_w(b + 1, 2, 3)
+            if b == 0:
+                zeros("d2")
+        t_lo = make_list(b + 1, [t_sv, t_ss], gap0, gap1, gap2)
+        t_w = now("vq", "vz")
+        t_n = own_numbers(b + 1, t_lo, t_n + now("sh"))
+        p = merge_list(b + 1, t_lo)
+        pick_v("o", "b%d" % (b + 1), 0, "b%d" % b, 0, mo(b), PL, free=True)
+        p[0]()
+        give_numbers(b + 1, t_n)
+        p[1]()
+        own(b + 1, t_lo)
+        p[2]()
+        if b == 0:
+            t_lw[2] = t_lw[2] + load_w("lw2b", 2, 2, 2, now("ls1", "li1"))
+            t_v = DMA(g.sync, "y", "lv", T.vt[:, :], T.v[:, :])
+            t_ia = [nought(T.ia[:, 0:PL], PL)]
+            nought(T.rb[:, :], CAP)
+            t_ih = [nought(T.ih[:, 0:PL], PL)]
+            nought(T.iw2[:, PL:W], CAP)
+            t_h.append([nought(T.h2[:, 0:128], 128)])
+            iota("sh", T.mr2[:, :], [[1, W]], 0, 0)
+            t_g[2] = gauge(2, "f")
+            zeros("c2")
+        else:
+            V("q", vec.quantize_mx, T.qv[:, :], T.sv[:, :], T.vt[:, :], deps=[t_v], free=True)
+            zeros("c3")
+        t_r, t_e = expert(b + 1, t_r + t_w)
+
+    t_mm = MM("st", T.psa, ("v", 0), ("c3", 0), [t_sv, t_ss])
+    take = take_numbers(2, kept_numbers(2))
+    take[0]()
+    DMA(g.sync, "y", "oc1", T.oc[:, 0:4 * PL], T.qc3[:, 0:PL].bitcast(dt.uint8), [t_sv])
+    t_n = count(2)
     for k in range(4):
-        DMA(g.sync, "y", "oc2", T.osc[4 * k:4 * k + 4, 0:PL], T.sf[32 * k:32 * k + 4, 0:96], [t_ss])
-    DMA(g.scalar, "s", "oc1", T.oc[:, 0:4 * PL], T.qf[:, 0:96].bitcast(dt.uint8), [t_sv])
+        DMA(g.sync if k < 2 else g.scalar, "y" if k < 2 else "s", "oc2", T.osc[4 * k:4 * k + 4, 0:PL], T.sc3[32 * k:32 * k + 4, 0:PL], [t_ss])
+    take[1]()
+    t_y = V("a", vec.tensor_copy, T.yb[:, :], T.psa[:, 0:PL], deps=[t_mm])
+    t_id = take[2]()
+    t_ks = V("f", vec.tensor_tensor, T.ksb[:, :], T.zc[:, PL - 1:W * L:W], T.km[:, :], OP.min, deps=[t_n])
     DMA(g.sync, "y", "oy", T.y[:, :], T.yb[:, :], [t_y])
-    for f in take_numbers(2):
-        f()
-    t_id = S("s3", T.idl[:, :], T.iw2[:, :].indirect(mo(2)), AF.Copy, deps=now("vi"))
     DMA(g.scalar, "s", "oi", T.ids[0:1, :], T.idl[0:1, :], [t_id])
-    V("f", vec.tensor_tensor, T.km[:, :], T.zc[:, 95:96 * L:96], T.ko[:, :], OP.min, deps=now("va"))
-    t_ks = V("f", vec.tensor_scalar, T.ksb[:, :], T.km[:, :], 256.0 * CAP, 1.0 / 256, OP.min, OP.mult)
     DMA(g.sync, "y", "ok", T.ks[0:1, :], T.ksb[0:1, :], [t_ks])
-    need("g", g, [(s, n) for s, n in cnt.items() if n] + [arr(f) for f in FLOWS])
+    need("g", g, [(s, n) for s, n in cnt.items() if n] + [cols(b) for b in range(L)] + [arr(f) for f in FLOWS if f[0] in "li"])

from concourse.bass import DstId, RemoteDMATransfer
from concourse.mybir import dt, AluOpType, ActivationFunctionType

PL, L, CAP = 96, 3, 32
W = PL + CAP
OP, AF = AluOpType, ActivationFunctionType
F8, U8, F32, BF, U16, I32 = "float8_e4m3fn_x4", "uint8", "float32", "bfloat16", "uint16", "int32"

SCRATCH = {}


def _buf(name, n, dtype, where="sbuf"):
    SCRATCH[name] = (where, [128, n], dtype)


def _pair(name, n):
    _buf("q" + name, n, F8)
    _buf("s" + name, n, U8)


for _n, _w in (("xt", 512), ("vt", 512), ("zt", 512), ("wt0", 2048), ("wt1", 2048), ("wt2", 2048), ("h0", 512), ("h1", 512), ("h2", 512),
               ("zc", W * L), ("wn", W), ("ex", W)):
    _buf(_n, _w, BF)
for _n, _w in (("g0", 128), ("g1", 128), ("g2", 128), ("w0", 512), ("w1", 512), ("w2", 512), ("v", 128),
               ("b0", 128), ("b1", 128), ("b2", 128), ("c0", 128), ("c1", 224), ("c2", 224), ("c3", 224),
               ("d0", 224), ("d1", 224), ("d2", 224), ("e0", 160), ("e1", 160), ("e2", 160)):
    _pair(_n, _w)
for _n in ("psa", "pr0", "pr1", "pr2", "pr3"):
    _buf(_n, 512, F32, "psum")
for _n, _w in (("t16", 96), ("row", W), ("cc", 4), ("mk", 96), ("rs", 96), ("one", W), ("jk", W * L), ("jk2", W * L), ("jk3", CAP * L), ("acc", 2 * L),
               ("mr0", W), ("mr1", W), ("mr2", W), ("ds", 96 * L),
               ("ia0", W), ("ia", W), ("iw0", W), ("iw1", W), ("iw2", W), ("ih", W), ("im", 96), ("idl", 96),
               ("sit1", 32), ("sit2", 32), ("rb", 32), ("his", L), ("km", L), ("ksb", L), ("yb", 96)):
    _buf(_n, _w, F32)
_buf("iq", 2, I32)
_buf("iqa", 2, I32)
_buf("cf", 8 * L, U16)
_buf("mo", 8 * L, U16)
_buf("lo", 2 * L, U16)
_buf("ll", 2 * L, U16)
for _b in range(L):
    _buf("xa%d" % _b, 48, F8)
    _buf("xb%d" % _b, 48, F8)
    _buf("xs%d" % _b, PL, U8)
_buf("xis", L, F32)
_buf("xls", 2 * L, U16)

FLOWS = {}
for _b in range(L):
    FLOWS["a%d" % _b] = (0, _b, "xa%d" % _b, 0, "qd%d" % _b, 0, 48)
    FLOWS["b%d" % _b] = (2, _b, "xb%d" % _b, 0, "qd%d" % _b, 48, 48)
    FLOWS["s%d" % _b] = (1, _b, "xs%d" % _b, 0, "sd%d" % _b, 0, PL)
    FLOWS["l%d" % _b] = (0, _b, "xls", 2 * _b, "ll", 2 * _b, 2)
    if _b:
        FLOWS["i%d" % _b] = (1, _b, "xis", _b, "his", _b, 1)
ORDER = (("a0", "l0", "a1", "l1", "a2", "l2"), ("s0", "s1", "i1", "s2", "i2"), ("b0", "b1", "b2"))

VCH, SCH = ["va", "vc", "ve", "vf", "vp", "vi", "vq", "vk", "vo", "vt", "vz"], ["s1", "s2", "s3", "s4"]
SEMAPHORES = (["a_" + f for f in FLOWS] + VCH + SCH + ["st", "r0", "r1", "r2", "r3", "sq", "sg", "sh", "lsa", "ls0", "ls1", "ls2", "li1", "li2", "lx", "lv",
              "oy", "oc1", "oc2", "oi", "ok", "lw0a", "lw0b", "lw1", "lw2a", "lw2b"])


def _raw(view, name):
    return view.bitcast(dt.uint8) if SCRATCH[name][2] == F8 else view


def _mask(es):
    return sum(1 << e for e in es)


def _landed(f):
    return "a_a" + f[1] if f[0] in "abs" else "a_" + f


def _relays(core, T, topo):
    r = T.rank_of(core)
    ps = [T.cores[r ^ (1 << b)] for b in range(L)]
    rel = [c for c in topo.cores_of(core) if c != core and all(topo.may_write(c, p) for p in ps)]
    rel.sort(key=lambda c: (topo.die(c) != topo.die(core), c))
    return rel[:3], ps


def _hop1(f, src, dst, topo):
    es = topo.engines(src, dst)
    h = len(es) // 2
    return es[:h] if f[0] == "a" else es[h:] if f[0] == "b" else es


def _relay_program(g, core, me, partners, T, topo, rankcore):
    sent = 0
    for f in ORDER[me]:
        _, lev, xb, xa, db, a, w = FLOWS[f]
        g.wait_ge(T.sem["a_" + f], len(_hop1(f, rankcore, core, topo)))
        dst = partners[lev]
        rid, pid = topo.addr(dst, core)
        es = topo.engines(core, dst)
        g.remote_dma(_raw(T[db][:, a:a + w], db), _raw(T[xb][:, xa:xa + w], xb), T.sem[_landed(f)], T.sem.lsa, pid, rid, _mask(es))
        sent += len(es)
    g.wait_ge(T.sem.lsa, sent)


def rank_program(g, core, T, topo):
    rank = T.rank_of(core)
    if rank is None:
        for rc in T.cores:
            if rc in topo.cores_of(core):
                rel, partners = _relays(rc, T, topo)
                if core in rel:
                    _relay_program(g, core, rel.index(core), partners, T, topo, rc)
        return
    rel, partners = _relays(core, T, topo)
    cnt = {}
    seen = {}
    vec = g.vector

    def need(q, eng, toks):
        best = {}
        for s, n in toks:
            if seen.get((q, s), 0) < n:
                best[s] = max(n, best.get(s, 0))
        for s in best:
            eng.wait_ge(T.sem[s], best[s])
            seen[(q, s)] = best[s]

    def bump(s, ins, n=1):
        ins.then_inc(T.sem[s], n)
        cnt[s] = cnt.get(s, 0) + n
        return (s, cnt[s])

    def now(*names):
        return [(s, cnt[s]) for s in names if cnt.get(s)]

    def V(ch, call, *args, deps=(), free=False, **kw):
        s = "v" + ch
        need("v", vec, ([] if free else now(s)) + list(deps))
        return bump(s, call(*args, **kw))

    def S(ch, *args, deps=(), free=False, **kw):
        need("s", g.scalar, ([] if free else now(ch)) + list(deps))
        return bump(ch, g.scalar.activation(*args, **kw))

    def MM(s, out, l, r, deps):
        need("t", g.tensor, deps)
        (ln, la), (rn, ra) = l, r
        return bump(s, g.tensor.matmul_mx(out[:, 0:128], T["q" + ln][:, la:la + 128], T["s" + ln][:, la:la + 128],
                                          T["q" + rn][:, ra:ra + 128], T["s" + rn][:, ra:ra + 128], True, True))

    def DMA(eng, q, s, out, in_, deps=()):
        need(q, eng, deps)
        return bump(s, eng.dma_start(out, in_), 16)

    def pick_s(ch, out, a, win, wa, off, w, deps=()):
        return S(ch, T["s" + out][:, a:a + w], T["s" + win][:, wa:wa + 128].indirect(off), AF.Copy, deps=deps)

    def pick_v(ch, out, a, win, wa, off, w, deps=(), free=False):
        return V(ch, vec.tensor_copy, T["q" + out][:, a:a + w].bitcast(dt.uint32), T["q" + win][:, wa:wa + 128].bitcast(dt.uint32).indirect(off),
                 deps=deps, free=free)

    def hop1(f, name, a):
        k, lev, xb, xa, _, _, w = FLOWS[f]
        rid, pid = topo.addr(rel[k], core)
        es = _hop1(f, core, rel[k], topo)
        gone = ("li%d" if f[0] == "i" else "ls%d") % lev
        cnt[gone] = cnt.get(gone, 0) + len(es)
        return rid, pid, _mask(es), _raw(T[xb][:, xa:xa + w], xb), _raw(T[name][:, a:a + w], name), gone

    def send(f, name, a, deps):
        need("g", g, deps)
        rid, pid, m, out, in_, gone = hop1(f, name, a)
        g.remote_dma(out, in_, T.sem["a_" + f], T.sem[gone], pid, rid, m)

    def send2(parts, deps):
        need("g", g, deps)
        tr = []
        for f, name, a in parts:
            rid, pid, m, out, in_, gone = hop1(f, name, a)
            tr.append(RemoteDMATransfer(dst_ids=[DstId(rid=rid, pnc=pid)], dma_engine_mask=m, remote_sem=T.sem["a_" + f], srcs=[in_], dsts=[out]))
        g.remote_dma_fused(tr, local_sem=T.sem[gone])

    def arr(*fs):
        src = _relays(partners[FLOWS[fs[0]][1]], T, topo)[0]
        return (_landed(fs[0]), sum(len(topo.engines(src[FLOWS[f][0]], core)) for f in fs))

    def cols(b):
        return arr("a%d" % b, "b%d" % b, "s%d" % b)

    def columns(b, tq, ts):
        send2([("a%d" % b, "qc%d" % b, 0), ("b%d" % b, "qc%d" % b, 48)], [tq])
        send("s%d" % b, "sc%d" % b, 0, [ts])

    def c(name, b, w=W):
        return T[name][:, w * b:w * b + w]

    def mo(b):
        return T.mo[:, 8 * b:8 * b + 6]

    def lo(b):
        return T.lo[:, 2 * b:2 * b + 2]

    def ll(b):
        return T.ll[:, 2 * b:2 * b + 2]

    DMA(g.sync, "y", "lx", T.xt[:, 0:4 * PL], T.x[:, 0:4 * PL])
    t_x = DMA(g.scalar, "s", "lx", T.xt[:, 4 * PL:4 * PL + 16], T.u[:, 0:16])

    def load_w(s, b, i, n, deps=()):
        return [DMA(g.sync, "y", s, T["wt%d" % b][:, 512 * i:512 * (i + n)], T.w[:, 2048 * b + 512 * i:2048 * b + 512 * (i + n)], deps)] * n
    t_lw = [load_w("lw0a", 0, 0, 2) + load_w("lw0b", 0, 2, 2), None, None]

    def iota(s, view, pattern, base, cm):
        return bump(s, g.iota(view, pattern, base, cm, allow_small_or_imprecise_dtypes=True))

    def nought(view, n):
        return iota("sh", view, [[0, n]], 0, 0)
    t_iq = bump("sq", g.iota(T.iq[:, 0:2], [[0, 2]], 0, 1))
    t_row = iota("sg", T.row[:, :], [[1, W]], 0, 0)
    t_io = iota("sg", T.t16[:, 0:96], [[0, 6], [1, 16]], 0, 0)

    def fill(view, val):
        return V("k", vec.memset, view, val, free=True)
    fill(T.xt[:, 4 * PL + 16:512], 0.0)
    fill(T.cf[:, 0:8], PL)
    fill(T.wn[:, PL:W], 0.0)
    ic, jb0, jb1, back = T.cc[:, 0:1], T.cc[:, 1:2], T.cc[:, 2:3], T.cc[:, 3:4]
    V("c", vec.tensor_scalar, T.iqa[:, :], T.iq[:, :], 15, None, OP.bitwise_and, deps=[t_iq])
    fill(T.ex[:, 0:PL], 0.0)
    fill(T.h0[:, 0:128], 0.0)
    t_ic = V("c", vec.tensor_copy, ic, T.iqa[:, 0:1])
    t_z = fill(T.zt[:, :], 0.0)
    V("t", vec.tensor_scalar, jb0, ic, 0.5, None, OP.add, deps=[t_ic])
    t_jc = V("t", vec.tensor_scalar, jb1, ic, 16.5, None, OP.add, free=True)
    V("k", vec.tensor_copy, T.ex[:, PL:W], T.row[:, 1:CAP + 1], deps=[t_row], free=True)
    t_k = now("vk")

    t_qc = V("c", vec.quantize_mx, T.qc0[:, :], T.sc0[:, :], T.xt[:, :], deps=t_k + [t_x])
    columns(0, t_qc, t_qc)

    def gauge(b, ch):
        off = T.cf[:, 8 * b:8 * b + 8]
        s = pick_s("s4", "g%d" % b, 0, "c0", 0, off, 128, now("vk") + [t_qc])
        return [pick_v(ch, "g%d" % b, 0, "c0", 0, off, 128, now("vk") + [t_qc]), s]
    V("o", vec.quantize_mx, T.qb0[:, :], T.sb0[:, :], T.xt[:, :], free=True)
    t_g = [gauge(0, "a"), None, None]

    def zeros(*names):
        for n in names:
            V("z", vec.quantize_mx, T["q" + n][:, 96:224], T["s" + n][:, 96:224], T.zt[:, :], deps=[t_z], free=True)

    def make_list(b, deps, gap0, gap1, gap2):
        t_mm = MM("st", T.psa, ("g%d" % b, 0), ("c%d" % b, 0), deps)
        gap0()
        V("a", vec.tensor_scalar, T.wn[:, 0:PL], T.psa[:, 0:PL], 0.0, None, OP.is_lt, deps=[t_mm])
        gap1()
        t_zc = V("a", vec.tensor_tensor_scan, c("zc", b), T.wn[:, :], T.ex[:, :], 0.0, OP.add, OP.max)
        a0 = S("s2", c("jk", b), c("zc", b), AF.Sign, bias=jb0, scale=-1.0, accum_out=T.acc[:, 2 * b:2 * b + 1], deps=[t_jc, t_zc], free=True)
        a1 = S("s2", c("jk2", b), c("zc", b), AF.Sign, bias=jb1, scale=-1.0, accum_out=T.acc[:, 2 * b + 1:2 * b + 2], free=True)
        gap2()
        t_lo = V("a", vec.tensor_scalar, lo(b), T.acc[:, 2 * b:2 * b + 2], float(W), 0.5, OP.add, OP.mult, deps=[a0, a1])
        send("l%d" % b, "lo", 2 * b, [t_lo])
        return t_lo

    def merge_list(b, t_lo):
        mr = T["mr%d" % b]
        return [lambda: V("p", vec.tensor_copy, mr[:, :].indirect(lo(b)), T.row[:, PL:W], deps=now("vt", "sh") + [t_lo]),
                lambda: V("p", vec.tensor_tensor_scan, c("ds", b, PL), T.rs[:, :], mr[:, 0:PL], 0.0, OP.add, OP.max),
                lambda: V("p", vec.tensor_scalar, mo(b), T.ds[:, 96 * b + 15:96 * b + 96:16], back, None, OP.add)]

    def own(b, t_lo):
        pick_v("o", "e%d" % b, 128, "c%d" % b, 0, lo(b), CAP, [t_lo], free=True)
        pick_s("s4", "e%d" % b, 128, "c%d" % b, 0, lo(b), CAP, [t_lo])

    def quant_w(b, *tiles):
        for i in tiles:
            V("q", vec.quantize_mx, T["qw%d" % b][:, 128 * i:128 * i + 128], T["sw%d" % b][:, 128 * i:128 * i + 128],
              T["wt%d" % b][:, 512 * i:512 * i + 512], deps=[t_lw[b][i]], free=True)

    def expert(b, deps):
        h, n = T["h%d" % b], PL
        tr = [MM("r%d" % i, T["pr%d" % i], ("w%d" % b, 128 * i), ("d%d" % b, 0), deps + [cols(b)]) for i in range(4)]
        S("s1", h[:, 128:512:4], T.pr0[:, 0:n], AF.Copy, scale=0.0625, deps=[tr[0]])
        t2 = S("s1", h[:, 130:512:4], T.pr2[:, 0:n], AF.Copy, scale=0.0625, deps=[tr[2]], free=True)
        need("s", g.scalar, now("vo", "vp", "s4"))
        V("e", vec.tensor_scalar, h[:, 129:512:4], T.pr1[:, 0:n], 0.0625, None, OP.mult, deps=[tr[1]], free=True)
        t3 = V("e", vec.tensor_scalar, h[:, 131:512:4], T.pr3[:, 0:n], 0.0625, None, OP.mult, deps=[tr[3]], free=True)
        need("v", vec, now("vk", "vo", "vp", "vc") + t_h[b])
        t_e = V("e", vec.quantize_mx, T["qe%d" % b][:, 0:128], T["se%d" % b][:, 0:128], h[:, :], deps=[t2, t3], free=True)
        return [t2, t3], t_e

    def ia(b):
        return T.ia if b else T.ia0

    def own_numbers(b, t_lo, deps):
        return S("s3", ia(b)[:, PL:W], T["iw%d" % b][:, :].indirect(lo(b)), AF.Copy, deps=deps + [t_lo])

    def give_numbers(b, t):
        send("i%d" % b, "sit%d" % b, 0, [V("i", vec.transpose, T["sit%d" % b][:, :], T.ia[:, PL:W], deps=[t])])

    def new_numbers(b, deps):
        S("s3", T["iw%d" % b][:, PL:W], ia(b)[:, :].indirect(ll(b)), AF.Copy, deps=deps)

    def kept_numbers(b):
        return S("s3", T.im[:, :] if b else T.iw1[:, 0:PL], T["iw%d" % b][:, :].indirect(mo(b)), AF.Copy)

    def count(b):
        return S("s4", c("jk3", b, CAP), T.one[:, :].indirect(ll(b)), AF.Copy, accum_out=T.km[:, b:b + 1], deps=now("vt"), free=True)

    def take_numbers(b, t_kept):
        out = T.iw2[:, 0:PL] if b == 1 else T.idl[:, :]
        return [lambda: V("i", vec.tensor_copy, T.rb[:, 0:1], T.his[:, b:b + 1], deps=t_ih + [arr("i%d" % b)]),
                lambda: V("i", vec.transpose, T.ih[:, PL:W], T.rb[:, :]),
                lambda: V("i", vec.tensor_tensor, out, T.ih[:, :].indirect(mo(b)), T.im[:, :], OP.add, deps=[t_kept])]

    def consts():
        t = V("t", vec.tensor_scalar, T.mk[:, :], T.t16[:, :], ic, -64.0 * W, OP.is_equal, OP.mult, deps=[t_io], free=True)
        V("t", vec.tensor_copy, T.mr0[:, :], T.row[:, :], free=True)
        V("t", vec.tensor_scalar, back, ic, -15.0, float(W), OP.add, OP.mult, free=True)
        V("t", vec.tensor_scalar, T.rs[:, :], T.mk[:, :], float(W), None, OP.add, deps=[t], free=True)
        V("t", vec.tensor_scalar, T.one[:, :], T.row[:, :], float(PL), None, OP.is_lt, free=True)

    def offsets():
        fill(T.cf[:, 8:16], PL + 1)
        fill(T.cf[:, 16:24], PL + 2)
    t_lo = make_list(0, [t_qc] + t_g[0], lambda: zeros("d0", "c1", "d1"), offsets, consts)
    t_lw[1] = load_w("lw1", 1, 0, 4, now("ls0"))
    t_lw[2] = load_w("lw2a", 2, 0, 2)

    p = merge_list(0, t_lo)
    quant_w(0, 0)
    p[0]()
    iota("sh", T.iw0[:, :], [[1, W]], rank * PL, 0)
    t_i0 = iota("sh", T.ia0[:, 0:PL], [[1, PL]], T.rank_of(partners[0]) * PL, 0)
    t_h = [[], [nought(T.h1[:, 0:128], 128)]]
    nought(T.iw1[:, PL:W], CAP)
    iota("sh", T.mr1[:, :], [[1, W]], 0, 0)
    quant_w(0, 1)
    p[1]()
    quant_w(0, 2, 3)
    t_w = now("vq", "vz")
    p[2]()
    own(0, t_lo)
    t_g[1] = gauge(1, "f")
    own_numbers(0, t_lo, [t_i0])
    t_r, t_e = expert(0, t_w)
    t_ia, t_ih = [], []

    for b in range(L):
        d = [arr("l%d" % b), t_e]
        pick_s("s1", "b%d" % b, PL, "e%d" % b, CAP, ll(b), CAP, d)
        pick_v("c", "b%d" % b, PL, "e%d" % b, CAP, ll(b), CAP, d)
        new_numbers(b, t_ia)
        need("t", g.tensor, now("vz", "va", "vq") + (t_g[b + 1] if b < 2 else []))
        t_ss = pick_s("s1", "c%d" % (b + 1), 0, "b%d" % b, 0, mo(b), PL)
        t_sv = pick_v("c", "c%d" % (b + 1), 0, "b%d" % b, 0, mo(b), PL)
        if b == 2:
            break
        columns(b + 1, t_sv, t_ss)
        t_n = [kept_numbers(b)]
        take = take_numbers(1, t_n[0])

        def gap0():
            pick_s("s4", "b%d" % (b + 1), 0, "b%d" % b, 0, mo(b), PL)
            count(b)
            quant_w(b + 1, 0, 1)
            if b == 1:
                take[0]()

        def gap1():
            if b == 1:
                take[1]()

        def gap2():
            if b == 1:
                t_n.append(take[2]())
            quant_w(b + 1, 2, 3)
            if b == 0:
                zeros("d2")
        t_lo = make_list(b + 1, [t_sv, t_ss], gap0, gap1, gap2)
        t_w = now("vq", "vz")
        t_n = own_numbers(b + 1, t_lo, t_n + now("sh"))
        p = merge_list(b + 1, t_lo)
        pick_v("o", "b%d" % (b + 1), 0, "b%d" % b, 0, mo(b), PL, free=True)
        p[0]()
        give_numbers(b + 1, t_n)
        p[1]()
        own(b + 1, t_lo)
        p[2]()
        if b == 0:
            t_lw[2] = t_lw[2] + load_w("lw2b", 2, 2, 2, now("ls1", "li1"))
            t_v = DMA(g.sync, "y", "lv", T.vt[:, :], T.v[:, :])
            t_ia = [nought(T.ia[:, 0:PL], PL)]
            nought(T.rb[:, :], CAP)
            t_ih = [nought(T.ih[:, 0:PL], PL)]
            nought(T.iw2[:, PL:W], CAP)
            t_h.append([nought(T.h2[:, 0:128], 128)])
            iota("sh", T.mr2[:, :], [[1, W]], 0, 0)
            t_g[2] = gauge(2, "f")
            zeros("c2")
        else:
            V("q", vec.quantize_mx, T.qv[:, :], T.sv[:, :], T.vt[:, :], deps=[t_v], free=True)
            zeros("c3")
        t_r, t_e = expert(b + 1, t_r + t_w)

    t_mm = MM("st", T.psa, ("v", 0), ("c3", 0), [t_sv, t_ss])
    take = take_numbers(2, kept_numbers(2))
    take[0]()
    DMA(g.sync, "y", "oc1", T.oc[:, 0:4 * PL], T.qc3[:, 0:PL].bitcast(dt.uint8), [t_sv])
    t_n = count(2)
    for k in range(4):
        DMA(g.sync if k < 2 else g.scalar, "y" if k < 2 else "s", "oc2", T.osc[4 * k:4 * k + 4, 0:PL], T.sc3[32 * k:32 * k + 4, 0:PL], [t_ss])
    take[1]()
    t_y = V("a", vec.tensor_copy, T.yb[:, :], T.psa[:, 0:PL], deps=[t_mm])
    t_id = take[2]()
    t_ks = V("f", vec.tensor_tensor, T.ksb[:, :], T.zc[:, PL - 1:W * L:W], T.km[:, :], OP.min, deps=[t_n])
    DMA(g.sync, "y", "oy", T.y[:, :], T.yb[:, :], [t_y])
    DMA(g.scalar, "s", "oi", T.ids[0:1, :], T.idl[0:1, :], [t_id])
    DMA(g.sync, "y", "ok", T.ks[0:1, :], T.ksb[0:1, :], [t_ks])
    need("g", g, [(s, n) for s, n in cnt.items() if n] + [cols(b) for b in range(L)] + [arr(f) for f in FLOWS if f[0] in "li"])
